import numpy as np
import ml_dtypes


def mxq(x, axis, fmt="e4m3"):
    dtype, down = {"e4m3": (ml_dtypes.float8_e4m3fn, 7), "e5m2": (ml_dtypes.float8_e5m2, 14)}[fmt]
    v = np.moveaxis(np.asarray(x, np.float32).astype(ml_dtypes.bfloat16).astype(np.float64), axis, -1)
    blocks = v.reshape(v.shape[:-1] + (-1, 32))
    amax = np.abs(blocks).max(-1, keepdims=True)
    byte = np.maximum(np.where(amax > 0, np.frexp(amax)[1] - 1 + 127, 0) - down, 1)
    scale = np.exp2(byte - 127.0)
    codes = (blocks / scale).astype(np.float32).astype(dtype).astype(np.float64)
    return np.moveaxis((codes * scale).reshape(v.shape), -1, axis)


WIDE = False


def mx_kscale(k):
    if not WIDE:
        return np.ones(k)
    levels = np.array([10, -10, 5, -5, 0])
    if k % 512:
        return np.exp2(np.random.permutation(np.resize(levels, k // 32))).repeat(32)
    a = np.empty((k // 512, 16))
    for p in range(k // 512):
        a[p, :8] = np.random.permutation(np.resize(levels, 8))
        for g in range(8):
            far = levels[np.abs(levels - a[p, g]) >= 10]
            a[p, g + 8] = far[np.random.randint(len(far))]
    return np.exp2(a.ravel()).repeat(32)


def f64(x):
    return np.asarray(x).astype(np.float64)


def striped(idx):
    return np.tile(idx.reshape(-1, 16).T, (8, 1)).astype(np.uint16)


def unstriped(offs):
    return offs[:16].T.reshape(-1).astype(np.int64)


def pack_weight(w):
    k, n = w.shape
    w = f64(np.asarray(w, np.float32).astype(ml_dtypes.bfloat16)).reshape(k // 32, 32, n)
    amax = np.abs(w).max(1)
    byte = np.clip(np.where(amax > 0, np.frexp(amax)[1] - 1 + 127 - 7, 1), 1, 254)
    scaled = (w * np.exp2(127.0 - byte)[:, None, :]).reshape(k, n).astype(np.float32)
    words = np.ascontiguousarray(scaled.reshape(k // 512, 128, 4, n).transpose(0, 1, 3, 2)).astype(ml_dtypes.float8_e4m3fn).view(np.uint8)
    return words, np.ascontiguousarray(byte.astype(np.uint8).reshape(k // 512, 16, n))


def unpack_weight(words, scales):
    g, p, n, _ = words.shape
    vals = np.ascontiguousarray(words).view(ml_dtypes.float8_e4m3fn).astype(np.float64) * np.repeat(np.exp2(scales.astype(np.float64) - 127.0), 8, axis=1)[..., None]
    return vals.transpose(0, 1, 3, 2).reshape(g * 512, n)


K, T, S, H, N = 512, 1024, 512, 512, 256


def setup_inputs():
    n = np.random.standard_normal
    s = mx_kscale(K)[:, None]
    u = mx_kscale(H)
    packed_xT = pack_weight(n((K, T)) * s)
    packed_w2 = pack_weight(n((H, N)) / np.sqrt(H) / u[:, None])
    return {
        "x_words": packed_xT[0],
        "x_scales": packed_xT[1],
        "w1": (n((K, H)) / np.sqrt(K) / s * u).astype(np.float32),
        "w2_words": packed_w2[0],
        "w2_scales": packed_w2[1],
        "offs": striped(np.random.permutation(T)[:S]),
    }


def reference(x_words, x_scales, w1, w2_words, w2_scales, offs):
    xq = unpack_weight(x_words, x_scales)[:, unstriped(offs)]
    h = mxq(f64(w1), 0, "e4m3").T @ xq
    z = h - h.mean(axis=1, keepdims=True)
    return unpack_weight(w2_words, w2_scales).T @ mxq(z, 0, "e4m3")

@@ -1,0 +1,112 @@
+from contextlib import ExitStack
+
+import concourse.mybir as mybir
+
+K, T, S, H, N = 512, 1024, 512, 512, 256
+FLOPS = 2 * K * H * S + 2 * H * N * S
+
+F32 = mybir.dt.float32
+BF16 = mybir.dt.bfloat16
+I32 = mybir.dt.int32
+U32 = mybir.dt.uint32
+U16 = mybir.dt.uint16
+U8 = mybir.dt.uint8
+FP8X4 = mybir.dt.float8_e4m3fn_x4
+MULT = mybir.AluOpType.mult
+ADD = mybir.AluOpType.add
+COPY = mybir.ActivationFunctionType.Copy
+
+P = 128
+PACK = 4
+BLOCK = 128
+M_VECTOR = 84
+
+
+def tile_picked_deepset_none_p_kernel(tc, x_words, x_scales, w1, w2_words, w2_scales, offs, out):
+    nc = tc.nc
+    with ExitStack() as ctx:
+        sb = ctx.enter_context(tc.tile_pool(name="sb", bufs=1))
+        ps = ctx.enter_context(tc.psum_pool(name="ps", bufs=1))
+
+        offsets = sb.tile([P, S // 16], U16, name="offsets")
+        w1_raw = sb.tile([P, PACK, H], F32, name="w1_raw", align_bytes=64)
+        xw = sb.tile([P, T], I32, name="xw", align_bytes=64)
+        xs = sb.tile([P, T], U8, name="xs", align_bytes=64)
+        w2w = sb.tile([P, N], I32, name="w2w", align_bytes=64)
+        w2s = sb.tile([P, N], U8, name="w2s", align_bytes=64)
+
+        nc.vector.memset(xs[:].bitcast(I32), 0)
+        nc.vector.memset(w2s[:].bitcast(I32), 0)
+        nc.sync.dma_start(out=w1_raw[:], in_=w1.rearrange("(p j) c -> p j c", j=PACK))
+        nc.sync.dma_start(offsets[:], offs)
+        for q in range(4):
+            nc.scalar.dma_start(out=xs[32 * q : 32 * q + 4, :].bitcast(I32), in_=x_scales[0, 4 * q : 4 * q + 4, :].bitcast(I32))
+        nc.sync.dma_start(out=xw[:], in_=x_words[0].rearrange("p c r -> p (c r)").bitcast(I32))
+        nc.sync.dma_start(out=w2w[:], in_=w2_words[0].rearrange("p c r -> p (c r)").bitcast(I32))
+        for q in range(4):
+            nc.sync.dma_start(out=w2s[32 * q : 32 * q + 4, :].bitcast(I32), in_=w2_scales[0, 4 * q : 4 * q + 4, :].bitcast(I32))
+
+        gs = sb.tile([P, S], U8, name="gs", align_bytes=64)
+        nc.vector.tensor_copy(gs[:], xs[:].indirect(offsets[:]))
+
+        wg = sb.tile([P, PACK, P, PACK], BF16, name="wg", align_bytes=64)
+        src = w1_raw[:].rearrange("p j (m t) -> p m j t", t=PACK)
+        dst = wg[:].rearrange("p t m j -> p m j t")
+        nc.vector.tensor_copy(out=dst[:, :M_VECTOR], in_=src[:, :M_VECTOR])
+        nc.scalar.copy(out=dst[:, M_VECTOR:], in_=src[:, M_VECTOR:])
+
+        wq = [sb.tile([P, P], U32, name="wq%d" % t, align_bytes=64) for t in range(PACK)]
+        wqs = [sb.tile([P, P], U8, name="wqs%d" % t, align_bytes=64) for t in range(PACK)]
+        gw = [sb.tile([P, S // 2], U32, name="gw%d" % u, align_bytes=64) for u in range(2)]
+        hb = [ps.tile([P, S], F32, name="hb%d" % t) for t in range(PACK)]
+
+        def quant_w(t):
+            nc.vector.quantize_mx(out=wq[t][:].bitcast(FP8X4), scales=wqs[t][:], in_=wg[:, t].rearrange("p m j -> p (m j)"))
+
+        def gather(u):
+            nc.vector.tensor_copy(gw[u][:], xw[:].bitcast(U32).indirect(offsets[:, 16 * u : 16 * u + 16]))
+
+        def mm1(t, u):
+            cols = slice(256 * u, 256 * u + 256)
+            nc.tensor.matmul_mx(out=hb[t][:, cols], lhsT=wq[t][:].bitcast(FP8X4), lhsT_scale=wqs[t][:],
+                                rhs=gw[u][:].bitcast(FP8X4), rhs_scale=gs[:, cols], start=True, stop=True)
+
+        gather(0)
+        for t in range(PACK):
+            quant_w(t)
+            mm1(t, 0)
+        gather(1)
+        for t in range(PACK):
+            mm1(t, 1)
+
+        hs = [sb.tile([P, S], F32, name="hs%d" % t, align_bytes=64) for t in range(PACK)]
+        negmean = [sb.tile([P, 1], F32, name="negmean%d" % t) for t in range(PACK)]
+        zp = sb.tile([P, PACK, S], BF16, name="zp", align_bytes=64)
+        for t in range(PACK):
+            if t == 1:
+                nc.vector.tensor_scalar(out=hs[t][:], in0=hb[t][:], scalar1=-1.0 / S, scalar2=None, op0=MULT, op1=ADD, accum_out=negmean[t][:])
+            else:
+                nc.scalar.activation(out=hs[t][:], in_=hb[t][:], func=COPY, scale=-1.0 / S, accum_out=negmean[t][:])
+            nc.vector.tensor_scalar(out=zp[:, t, :], in0=hs[t][:], scalar1=-float(S), scalar2=negmean[t][:], op0=MULT, op1=ADD)
+
+        out_v = out.rearrange("(a p) j -> p a j", p=P)
+        for b in range(S // BLOCK):
+            cols = slice(b * BLOCK, (b + 1) * BLOCK)
+            zg = sb.tile([P, BLOCK, PACK], BF16, name="zg%d" % b, align_bytes=64)
+            zsrc = zp[:, :, cols].rearrange("p t (c i) -> p c t i", i=4)
+            zdst = zg[:].rearrange("p (c i) t -> p c t i", i=4)
+            if b == 1:
+                nc.scalar.copy(out=zdst, in_=zsrc)
+            else:
+                nc.vector.tensor_copy(out=zdst, in_=zsrc)
+            zq = sb.tile([P, BLOCK], U32, name="zq%d" % b, align_bytes=64)
+            zs = sb.tile([P, BLOCK], U8, name="zs%d" % b, align_bytes=64)
+            nc.vector.quantize_mx(out=zq[:].bitcast(FP8X4), scales=zs[:], in_=zg[:].rearrange("p c t -> p (c t)"))
+            ob = ps.tile([P, 2, BLOCK], F32, name="ob%d" % b)
+            for a in range(2):
+                mc = slice(a * P, (a + 1) * P)
+                nc.tensor.matmul_mx(out=ob[:, a, :], lhsT=w2w[:, mc].bitcast(FP8X4), lhsT_scale=w2s[:, mc],
+                                    rhs=zq[:].bitcast(FP8X4), rhs_scale=zs[:], start=True, stop=True)
+            res = sb.tile([P, 2, BLOCK], F32, name="res%d" % b, align_bytes=64)
+            nc.scalar.copy(out=res[:], in_=ob[:])
+            nc.sync.dma_start(out=out_v[:, :, cols], in_=res[:])

@@ -19,7 +19,7 @@ COPY = mybir.ActivationFunctionType.Copy
 P = 128
 PACK = 4
 BLOCK = 128
-M_VECTOR = 84
+HALF = S // 2
 
 
 def tile_picked_deepset_none_p_kernel(tc, x_words, x_scales, w1, w2_words, w2_scales, offs, out):
@@ -29,18 +29,24 @@ def tile_picked_deepset_none_p_kernel(tc, x_words, x_scales, w1, w2_words, w2_sc
         ps = ctx.enter_context(tc.psum_pool(name="ps", bufs=1))
 
         offsets = sb.tile([P, S // 16], U16, name="offsets")
-        w1_raw = sb.tile([P, PACK, H], F32, name="w1_raw", align_bytes=64)
-        xw = sb.tile([P, T], I32, name="xw", align_bytes=64)
+        w1_raw = [sb.tile([P, 2, H], F32, name="w1_raw%d" % u, align_bytes=64) for u in range(2)]
+        xw = sb.tile([P, T], I32, name="xw", tag="window", align_bytes=64)
         xs = sb.tile([P, T], U8, name="xs", align_bytes=64)
         w2w = sb.tile([P, N], I32, name="w2w", align_bytes=64)
         w2s = sb.tile([P, N], U8, name="w2s", align_bytes=64)
 
         nc.vector.memset(xs[:].bitcast(I32), 0)
         nc.vector.memset(w2s[:].bitcast(I32), 0)
-        nc.sync.dma_start(out=w1_raw[:], in_=w1.rearrange("(p j) c -> p j c", j=PACK))
+        warm_in = sb.tile([P, 1], F32, name="warm_in")
+        warm_out = sb.tile([P, 1], F32, name="warm_out")
+        nc.gpsimd.memset(warm_in[:], 0.0)
+        nc.scalar.activation(out=warm_out[:], in_=warm_in[:], func=COPY, scale=-1.0 / S)
+        w1_v = w1.rearrange("(p j) c -> p j c", j=PACK)
+        nc.sync.dma_start(out=w1_raw[0][:], in_=w1_v[:, 0:2])
         nc.sync.dma_start(offsets[:], offs)
         for q in range(4):
-            nc.scalar.dma_start(out=xs[32 * q : 32 * q + 4, :].bitcast(I32), in_=x_scales[0, 4 * q : 4 * q + 4, :].bitcast(I32))
+            nc.sync.dma_start(out=xs[32 * q : 32 * q + 4, :].bitcast(I32), in_=x_scales[0, 4 * q : 4 * q + 4, :].bitcast(I32))
+        nc.sync.dma_start(out=w1_raw[1][:], in_=w1_v[:, 2:4])
         nc.sync.dma_start(out=xw[:], in_=x_words[0].rearrange("p c r -> p (c r)").bitcast(I32))
         nc.sync.dma_start(out=w2w[:], in_=w2_words[0].rearrange("p c r -> p (c r)").bitcast(I32))
         for q in range(4):
@@ -49,64 +55,82 @@ def tile_picked_deepset_none_p_kernel(tc, x_words, x_scales, w1, w2_words, w2_sc
         gs = sb.tile([P, S], U8, name="gs", align_bytes=64)
         nc.vector.tensor_copy(gs[:], xs[:].indirect(offsets[:]))
 
-        wg = sb.tile([P, PACK, P, PACK], BF16, name="wg", align_bytes=64)
-        src = w1_raw[:].rearrange("p j (m t) -> p m j t", t=PACK)
-        dst = wg[:].rearrange("p t m j -> p m j t")
-        nc.vector.tensor_copy(out=dst[:, :M_VECTOR], in_=src[:, :M_VECTOR])
-        nc.scalar.copy(out=dst[:, M_VECTOR:], in_=src[:, M_VECTOR:])
+        wg = [sb.tile([P, 2, P, PACK], BF16, name="wg%d" % u, align_bytes=64) for u in range(2)]
+        src = [w1_raw[u][:].rearrange("p j (m t) -> p m j t", t=PACK) for u in range(2)]
+        dst = [wg[u][:].rearrange("p t m j -> p m j t") for u in range(2)]
+        nc.scalar.copy(out=dst[0][:, :, 0:2], in_=src[0][:, :, :, 0:2])
+        nc.scalar.copy(out=dst[1][:, :, 0:2], in_=src[0][:, :, :, 2:4])
+        nc.vector.tensor_copy(out=dst[0][:, :, 2:4], in_=src[1][:, :, :, 0:2])
+        nc.scalar.copy(out=dst[1][:, :, 2:4], in_=src[1][:, :, :, 2:4])
 
-        wq = [sb.tile([P, P], U32, name="wq%d" % t, align_bytes=64) for t in range(PACK)]
-        wqs = [sb.tile([P, P], U8, name="wqs%d" % t, align_bytes=64) for t in range(PACK)]
-        gw = [sb.tile([P, S // 2], U32, name="gw%d" % u, align_bytes=64) for u in range(2)]
+        wq = [sb.tile([P, 2 * P], U32, name="wq0", align_bytes=64), None]
+        wqs = [sb.tile([P, 2 * P], U8, name="wqs%d" % u, align_bytes=64) for u in range(2)]
+        gw = sb.tile([P, S], U32, name="gw", align_bytes=64)
         hb = [ps.tile([P, S], F32, name="hb%d" % t) for t in range(PACK)]
 
-        def quant_w(t):
-            nc.vector.quantize_mx(out=wq[t][:].bitcast(FP8X4), scales=wqs[t][:], in_=wg[:, t].rearrange("p m j -> p (m j)"))
+        def quant_w(u):
+            nc.vector.quantize_mx(out=wq[u][:].bitcast(FP8X4), scales=wqs[u][:], in_=wg[u][:].rearrange("p t m j -> p (t m j)"))
 
-        def gather(u):
-            nc.vector.tensor_copy(gw[u][:], xw[:].bitcast(U32).indirect(offsets[:, 16 * u : 16 * u + 16]))
+        def gather(lo, hi):
+            nc.vector.tensor_copy(gw[:, lo:hi], xw[:].bitcast(U32).indirect(offsets[:, lo // 16 : hi // 16]))
 
-        def mm1(t, u):
-            cols = slice(256 * u, 256 * u + 256)
-            nc.tensor.matmul_mx(out=hb[t][:, cols], lhsT=wq[t][:].bitcast(FP8X4), lhsT_scale=wqs[t][:],
-                                rhs=gw[u][:].bitcast(FP8X4), rhs_scale=gs[:, cols], start=True, stop=True)
+        def mm1(t, lo, hi):
+            nc.tensor.matmul_mx(out=hb[t][:, lo:hi], lhsT=wq[t // 2][:, (t % 2) * P : (t % 2 + 1) * P].bitcast(FP8X4), lhsT_scale=wqs[t // 2][:, (t % 2) * P : (t % 2 + 1) * P],
+                                rhs=gw[:, lo:hi].bitcast(FP8X4), rhs_scale=gs[:, lo:hi], start=True, stop=True)
 
-        gather(0)
-        for t in range(PACK):
-            quant_w(t)
-            mm1(t, 0)
-        gather(1)
-        for t in range(PACK):
-            mm1(t, 1)
+        quant_w(0)
+        gather(0, HALF)
+        mm1(0, 0, HALF)
+        mm1(1, 0, HALF)
+        gather(HALF, S)
+        mm1(0, HALF, S)
+        mm1(1, HALF, S)
+        wq[1] = sb.tile([P, 2 * P], U32, name="wq1", tag="window", align_bytes=64)
+        quant_w(1)
+        mm1(2, 0, S)
+        mm1(3, 0, S)
 
         hs = [sb.tile([P, S], F32, name="hs%d" % t, align_bytes=64) for t in range(PACK)]
         negmean = [sb.tile([P, 1], F32, name="negmean%d" % t) for t in range(PACK)]
-        zp = sb.tile([P, PACK, S], BF16, name="zp", align_bytes=64)
+        zp = sb.tile([P, 2, S, 2], BF16, name="zp", align_bytes=64)
         for t in range(PACK):
             if t == 1:
                 nc.vector.tensor_scalar(out=hs[t][:], in0=hb[t][:], scalar1=-1.0 / S, scalar2=None, op0=MULT, op1=ADD, accum_out=negmean[t][:])
             else:
                 nc.scalar.activation(out=hs[t][:], in_=hb[t][:], func=COPY, scale=-1.0 / S, accum_out=negmean[t][:])
-            nc.vector.tensor_scalar(out=zp[:, t, :], in0=hs[t][:], scalar1=-float(S), scalar2=negmean[t][:], op0=MULT, op1=ADD)
+        for t in range(PACK):
+            nc.vector.tensor_scalar(out=zp[:, t // 2, :, t % 2], in0=hs[t][:], scalar1=-float(S), scalar2=negmean[t][:], op0=MULT, op1=ADD)
 
+        zwords = zp[:].rearrange("p u c e -> p u (c e)").bitcast(F32)
         out_v = out.rearrange("(a p) j -> p a j", p=P)
+        zg = []
         for b in range(S // BLOCK):
             cols = slice(b * BLOCK, (b + 1) * BLOCK)
-            zg = sb.tile([P, BLOCK, PACK], BF16, name="zg%d" % b, align_bytes=64)
-            zsrc = zp[:, :, cols].rearrange("p t (c i) -> p c t i", i=4)
-            zdst = zg[:].rearrange("p (c i) t -> p c t i", i=4)
-            if b == 1:
+            zg.append(sb.tile([P, BLOCK * PACK], BF16, name="zg%d" % b, align_bytes=64))
+            zsrc = zwords[:, :, cols].rearrange("p u c -> p c u")
+            zdst = zg[b][:].bitcast(F32).rearrange("p (c u) -> p c u", u=2)
+            if b >= 2:
                 nc.scalar.copy(out=zdst, in_=zsrc)
             else:
                 nc.vector.tensor_copy(out=zdst, in_=zsrc)
+        for b in range(S // BLOCK):
+            cols = slice(b * BLOCK, (b + 1) * BLOCK)
             zq = sb.tile([P, BLOCK], U32, name="zq%d" % b, align_bytes=64)
             zs = sb.tile([P, BLOCK], U8, name="zs%d" % b, align_bytes=64)
-            nc.vector.quantize_mx(out=zq[:].bitcast(FP8X4), scales=zs[:], in_=zg[:].rearrange("p c t -> p (c t)"))
+            nc.vector.quantize_mx(out=zq[:].bitcast(FP8X4), scales=zs[:], in_=zg[b][:])
             ob = ps.tile([P, 2, BLOCK], F32, name="ob%d" % b)
+            if b == 3:
+                ob2 = ps.tile([P, BLOCK], F32, name="ob_last", tag="hb0")
             for a in range(2):
                 mc = slice(a * P, (a + 1) * P)
-                nc.tensor.matmul_mx(out=ob[:, a, :], lhsT=w2w[:, mc].bitcast(FP8X4), lhsT_scale=w2s[:, mc],
+                nc.tensor.matmul_mx(out=ob2[:] if (b, a) == (3, 1) else ob[:, a, :], lhsT=w2w[:, mc].bitcast(FP8X4), lhsT_scale=w2s[:, mc],
                                     rhs=zq[:].bitcast(FP8X4), rhs_scale=zs[:], start=True, stop=True)
             res = sb.tile([P, 2, BLOCK], F32, name="res%d" % b, align_bytes=64)
-            nc.scalar.copy(out=res[:], in_=ob[:])
+            if b == 3:
+                nc.scalar.copy(out=res[:, 0], in_=ob[:, 0])
+                nc.vector.tensor_copy(out=res[:, 1], in_=ob2[:])
+            elif b % 2 == 0:
+                nc.scalar.copy(out=res[:], in_=ob[:])
+            else:
+                nc.vector.tensor_copy(out=res[:], in_=ob[:])
             nc.sync.dma_start(out=out_v[:, :, cols], in_=res[:])

@@ -67,6 +67,7 @@ def tile_picked_deepset_none_p_kernel(tc, x_words, x_scales, w1, w2_words, w2_sc
         wqs = [sb.tile([P, 2 * P], U8, name="wqs%d" % u, align_bytes=64) for u in range(2)]
         gw = sb.tile([P, S], U32, name="gw", align_bytes=64)
         hb = [ps.tile([P, S], F32, name="hb%d" % t) for t in range(PACK)]
+        hb1_first = ps.tile([P, HALF], F32, name="hb1_first")
 
         def quant_w(u):
             nc.vector.quantize_mx(out=wq[u][:].bitcast(FP8X4), scales=wqs[u][:], in_=wg[u][:].rearrange("p t m j -> p (t m j)"))
@@ -75,7 +76,7 @@ def tile_picked_deepset_none_p_kernel(tc, x_words, x_scales, w1, w2_words, w2_sc
             nc.vector.tensor_copy(gw[:, lo:hi], xw[:].bitcast(U32).indirect(offsets[:, lo // 16 : hi // 16]))
 
         def mm1(t, lo, hi):
-            nc.tensor.matmul_mx(out=hb[t][:, lo:hi], lhsT=wq[t // 2][:, (t % 2) * P : (t % 2 + 1) * P].bitcast(FP8X4), lhsT_scale=wqs[t // 2][:, (t % 2) * P : (t % 2 + 1) * P],
+            nc.tensor.matmul_mx(out=hb1_first[:] if (t, hi) == (1, HALF) else hb[t][:, lo:hi], lhsT=wq[t // 2][:, (t % 2) * P : (t % 2 + 1) * P].bitcast(FP8X4), lhsT_scale=wqs[t // 2][:, (t % 2) * P : (t % 2 + 1) * P],
                                 rhs=gw[:, lo:hi].bitcast(FP8X4), rhs_scale=gs[:, lo:hi], start=True, stop=True)
 
         quant_w(0)
@@ -92,24 +93,33 @@ def tile_picked_deepset_none_p_kernel(tc, x_words, x_scales, w1, w2_words, w2_sc
 
         hs = [sb.tile([P, S], F32, name="hs%d" % t, align_bytes=64) for t in range(PACK)]
         negmean = [sb.tile([P, 1], F32, name="negmean%d" % t) for t in range(PACK)]
-        zp = sb.tile([P, 2, S, 2], BF16, name="zp", align_bytes=64)
+        zp = sb.tile([P, S // BLOCK, 2, BLOCK, 2], BF16, name="zp", align_bytes=64)
+        part = sb.tile([P, 1], F32, name="part")
+        nc.scalar.activation(out=hs[1][:, :HALF], in_=hb1_first[:], func=COPY, scale=-1.0 / S, accum_out=part[:])
         for t in range(PACK):
             if t == 1:
-                nc.vector.tensor_scalar(out=hs[t][:], in0=hb[t][:], scalar1=-1.0 / S, scalar2=None, op0=MULT, op1=ADD, accum_out=negmean[t][:])
+                nc.vector.tensor_scalar(out=hs[t][:, HALF:], in0=hb[t][:, HALF:], scalar1=-1.0 / S, scalar2=part[:], op0=MULT, op1=ADD, accum_out=negmean[t][:])
             else:
                 nc.scalar.activation(out=hs[t][:], in_=hb[t][:], func=COPY, scale=-1.0 / S, accum_out=negmean[t][:])
-        for t in range(PACK):
-            nc.vector.tensor_scalar(out=zp[:, t // 2, :, t % 2], in0=hs[t][:], scalar1=-float(S), scalar2=negmean[t][:], op0=MULT, op1=ADD)
+        def centre(t, lo, hi):
+            nc.vector.tensor_scalar(out=zp[:, lo:hi, t // 2, :, t % 2], in0=hs[t][:].rearrange("p (b c) -> p b c", c=BLOCK)[:, lo:hi],
+                                    scalar1=-float(S), scalar2=negmean[t][:], op0=MULT, op1=ADD)
 
-        zwords = zp[:].rearrange("p u c e -> p u (c e)").bitcast(F32)
+        for t in range(PACK - 1):
+            centre(t, 0, 4)
+        for lo, hi in ((0, 1), (1, 2), (2, 4)):
+            centre(3, lo, hi)
+
+        zwords = zp[:].rearrange("p b u c e -> p b u (c e)").bitcast(F32)
+        banks = ["ob0", "ob1", "ob2", "hb1_first", "hb0", "hb1", "hb2", "hb3"]
         out_v = out.rearrange("(a p) j -> p a j", p=P)
         zg = []
         for b in range(S // BLOCK):
             cols = slice(b * BLOCK, (b + 1) * BLOCK)
             zg.append(sb.tile([P, BLOCK * PACK], BF16, name="zg%d" % b, align_bytes=64))
-            zsrc = zwords[:, :, cols].rearrange("p u c -> p c u")
+            zsrc = zwords[:, b].rearrange("p u c -> p c u")
             zdst = zg[b][:].bitcast(F32).rearrange("p (c u) -> p c u", u=2)
-            if b >= 2:
+            if b in (0, 1):
                 nc.scalar.copy(out=zdst, in_=zsrc)
             else:
                 nc.vector.tensor_copy(out=zdst, in_=zsrc)
@@ -118,19 +128,14 @@ def tile_picked_deepset_none_p_kernel(tc, x_words, x_scales, w1, w2_words, w2_sc
             zq = sb.tile([P, BLOCK], U32, name="zq%d" % b, align_bytes=64)
             zs = sb.tile([P, BLOCK], U8, name="zs%d" % b, align_bytes=64)
             nc.vector.quantize_mx(out=zq[:].bitcast(FP8X4), scales=zs[:], in_=zg[b][:])
-            ob = ps.tile([P, 2, BLOCK], F32, name="ob%d" % b)
-            if b == 3:
-                ob2 = ps.tile([P, BLOCK], F32, name="ob_last", tag="hb0")
+            res = sb.tile([P, 2, BLOCK], F32, name="res%d" % b, align_bytes=64)
             for a in range(2):
                 mc = slice(a * P, (a + 1) * P)
-                nc.tensor.matmul_mx(out=ob2[:] if (b, a) == (3, 1) else ob[:, a, :], lhsT=w2w[:, mc].bitcast(FP8X4), lhsT_scale=w2s[:, mc],
+                ob = ps.tile([P, BLOCK], F32, name="ob%d%d" % (b, a), tag=banks[2 * b + a])
+                nc.tensor.matmul_mx(out=ob[:], lhsT=w2w[:, mc].bitcast(FP8X4), lhsT_scale=w2s[:, mc],
                                     rhs=zq[:].bitcast(FP8X4), rhs_scale=zs[:], start=True, stop=True)
-            res = sb.tile([P, 2, BLOCK], F32, name="res%d" % b, align_bytes=64)
-            if b == 3:
-                nc.scalar.copy(out=res[:, 0], in_=ob[:, 0])
-                nc.vector.tensor_copy(out=res[:, 1], in_=ob2[:])
-            elif b % 2 == 0:
-                nc.scalar.copy(out=res[:], in_=ob[:])
-            else:
-                nc.vector.tensor_copy(out=res[:], in_=ob[:])
+                if a == 0 or b == 0:
+                    nc.scalar.copy(out=res[:, a], in_=ob[:])
+                else:
+                    nc.vector.tensor_copy(out=res[:, a], in_=ob[:])
             nc.sync.dma_start(out=out_v[:, :, cols], in_=res[:])

@@ -18,8 +18,14 @@ COPY = mybir.ActivationFunctionType.Copy
 
 P = 128
 PACK = 4
-BLOCK = 128
+QUADRANTS = 4
+LIST_ROWS = 16
 HALF = S // 2
+BLOCK = 128
+BLOCKS = S // BLOCK
+OUT_TILES = N // P
+SPLIT_TILE = 1
+SCALAR_WEAVES = 3
 
 
 def tile_picked_deepset_none_p_kernel(tc, x_words, x_scales, w1, w2_words, w2_scales, offs, out):
@@ -28,7 +34,7 @@ def tile_picked_deepset_none_p_kernel(tc, x_words, x_scales, w1, w2_words, w2_sc
         sb = ctx.enter_context(tc.tile_pool(name="sb", bufs=1))
         ps = ctx.enter_context(tc.psum_pool(name="ps", bufs=1))
 
-        offsets = sb.tile([P, S // 16], U16, name="offsets")
+        offsets = sb.tile([P, S // LIST_ROWS], U16, name="offsets")
         w1_raw = [sb.tile([P, 2, H], F32, name="w1_raw%d" % u, align_bytes=64) for u in range(2)]
         xw = sb.tile([P, T], I32, name="xw", tag="window", align_bytes=64)
         xs = sb.tile([P, T], U8, name="xs", align_bytes=64)
@@ -41,101 +47,125 @@ def tile_picked_deepset_none_p_kernel(tc, x_words, x_scales, w1, w2_words, w2_sc
         warm_out = sb.tile([P, 1], F32, name="warm_out")
         nc.gpsimd.memset(warm_in[:], 0.0)
         nc.scalar.activation(out=warm_out[:], in_=warm_in[:], func=COPY, scale=-1.0 / S)
-        w1_v = w1.rearrange("(p j) c -> p j c", j=PACK)
-        nc.sync.dma_start(out=w1_raw[0][:], in_=w1_v[:, 0:2])
+
+        def load_scale_rows(tile, rows):
+            for q in range(QUADRANTS):
+                nc.sync.dma_start(out=tile[32 * q : 32 * q + 4, :].bitcast(I32), in_=rows[4 * q : 4 * q + 4, :].bitcast(I32))
+
+        w1_rows = w1.rearrange("(p r) i -> p r i", r=PACK)
+        nc.sync.dma_start(out=w1_raw[0][:], in_=w1_rows[:, 0:2])
         nc.sync.dma_start(offsets[:], offs)
-        for q in range(4):
-            nc.sync.dma_start(out=xs[32 * q : 32 * q + 4, :].bitcast(I32), in_=x_scales[0, 4 * q : 4 * q + 4, :].bitcast(I32))
-        nc.sync.dma_start(out=w1_raw[1][:], in_=w1_v[:, 2:4])
+        load_scale_rows(xs, x_scales[0])
+        nc.sync.dma_start(out=w1_raw[1][:], in_=w1_rows[:, 2:4])
         nc.sync.dma_start(out=xw[:], in_=x_words[0].rearrange("p c r -> p (c r)").bitcast(I32))
         nc.sync.dma_start(out=w2w[:], in_=w2_words[0].rearrange("p c r -> p (c r)").bitcast(I32))
-        for q in range(4):
-            nc.sync.dma_start(out=w2s[32 * q : 32 * q + 4, :].bitcast(I32), in_=w2_scales[0, 4 * q : 4 * q + 4, :].bitcast(I32))
+        load_scale_rows(w2s, w2_scales[0])
 
-        gs = sb.tile([P, S], U8, name="gs", align_bytes=64)
-        nc.vector.tensor_copy(gs[:], xs[:].indirect(offsets[:]))
+        picked_scales = sb.tile([P, S], U8, name="picked_scales", align_bytes=64)
+        nc.vector.tensor_copy(picked_scales[:], xs[:].indirect(offsets[:]))
 
-        wg = [sb.tile([P, 2, P, PACK], BF16, name="wg%d" % u, align_bytes=64) for u in range(2)]
-        src = [w1_raw[u][:].rearrange("p j (m t) -> p m j t", t=PACK) for u in range(2)]
-        dst = [wg[u][:].rearrange("p t m j -> p m j t") for u in range(2)]
-        nc.scalar.copy(out=dst[0][:, :, 0:2], in_=src[0][:, :, :, 0:2])
-        nc.scalar.copy(out=dst[1][:, :, 0:2], in_=src[0][:, :, :, 2:4])
-        nc.vector.tensor_copy(out=dst[0][:, :, 2:4], in_=src[1][:, :, :, 0:2])
-        nc.scalar.copy(out=dst[1][:, :, 2:4], in_=src[1][:, :, :, 2:4])
+        w1_bf = [sb.tile([P, 2, P, PACK], BF16, name="w1_bf%d" % v, align_bytes=64) for v in range(2)]
+        cast_in = [w1_raw[u][:].rearrange("p r (m t) -> p m r t", t=PACK) for u in range(2)]
+        cast_out = [w1_bf[v][:].rearrange("p e m r -> p m r e") for v in range(2)]
+        nc.scalar.copy(out=cast_out[0][:, :, 0:2], in_=cast_in[0][:, :, :, 0:2])
+        nc.scalar.copy(out=cast_out[1][:, :, 0:2], in_=cast_in[0][:, :, :, 2:4])
+        nc.vector.tensor_copy(out=cast_out[0][:, :, 2:4], in_=cast_in[1][:, :, :, 0:2])
+        nc.scalar.copy(out=cast_out[1][:, :, 2:4], in_=cast_in[1][:, :, :, 2:4])
 
-        wq = [sb.tile([P, 2 * P], U32, name="wq0", align_bytes=64), None]
-        wqs = [sb.tile([P, 2 * P], U8, name="wqs%d" % u, align_bytes=64) for u in range(2)]
-        gw = sb.tile([P, S], U32, name="gw", align_bytes=64)
-        hb = [ps.tile([P, S], F32, name="hb%d" % t) for t in range(PACK)]
-        hb1_first = ps.tile([P, HALF], F32, name="hb1_first")
+        w1_codes = [sb.tile([P, 2 * P], U32, name="w1_codes0", align_bytes=64)]
+        w1_scales = [sb.tile([P, 2 * P], U8, name="w1_scales%d" % v, align_bytes=64) for v in range(2)]
+        picked_words = sb.tile([P, S], U32, name="picked_words", align_bytes=64)
+        h_bank = [ps.tile([P, S], F32, name="h_bank%d" % t) for t in range(PACK)]
+        h_split_first = ps.tile([P, HALF], F32, name="h_split_first")
 
-        def quant_w(u):
-            nc.vector.quantize_mx(out=wq[u][:].bitcast(FP8X4), scales=wqs[u][:], in_=wg[u][:].rearrange("p t m j -> p (t m j)"))
+        def quantise_w1(v):
+            nc.vector.quantize_mx(out=w1_codes[v][:].bitcast(FP8X4), scales=w1_scales[v][:], in_=w1_bf[v][:].rearrange("p e m r -> p (e m r)"))
 
-        def gather(lo, hi):
-            nc.vector.tensor_copy(gw[:, lo:hi], xw[:].bitcast(U32).indirect(offsets[:, lo // 16 : hi // 16]))
+        def gather_words(lo, hi):
+            nc.vector.tensor_copy(picked_words[:, lo:hi], xw[:].bitcast(U32).indirect(offsets[:, lo // LIST_ROWS : hi // LIST_ROWS]))
 
-        def mm1(t, lo, hi):
-            nc.tensor.matmul_mx(out=hb1_first[:] if (t, hi) == (1, HALF) else hb[t][:, lo:hi], lhsT=wq[t // 2][:, (t % 2) * P : (t % 2 + 1) * P].bitcast(FP8X4), lhsT_scale=wqs[t // 2][:, (t % 2) * P : (t % 2 + 1) * P],
-                                rhs=gw[:, lo:hi].bitcast(FP8X4), rhs_scale=gs[:, lo:hi], start=True, stop=True)
+        def first_product(t, lo, hi):
+            channels = slice((t % 2) * P, (t % 2 + 1) * P)
+            nc.tensor.matmul_mx(
+                out=h_split_first[:] if (t, hi) == (SPLIT_TILE, HALF) else h_bank[t][:, lo:hi],
+                lhsT=w1_codes[t // 2][:, channels].bitcast(FP8X4),
+                lhsT_scale=w1_scales[t // 2][:, channels],
+                rhs=picked_words[:, lo:hi].bitcast(FP8X4),
+                rhs_scale=picked_scales[:, lo:hi],
+                start=True,
+                stop=True,
+            )
 
-        quant_w(0)
-        gather(0, HALF)
-        mm1(0, 0, HALF)
-        mm1(1, 0, HALF)
-        gather(HALF, S)
-        mm1(0, HALF, S)
-        mm1(1, HALF, S)
-        wq[1] = sb.tile([P, 2 * P], U32, name="wq1", tag="window", align_bytes=64)
-        quant_w(1)
-        mm1(2, 0, S)
-        mm1(3, 0, S)
+        quantise_w1(0)
+        for lo in (0, HALF):
+            gather_words(lo, lo + HALF)
+            first_product(0, lo, lo + HALF)
+            first_product(1, lo, lo + HALF)
+        w1_codes.append(sb.tile([P, 2 * P], U32, name="w1_codes1", tag="window", align_bytes=64))
+        quantise_w1(1)
+        first_product(2, 0, S)
+        first_product(3, 0, S)
 
-        hs = [sb.tile([P, S], F32, name="hs%d" % t, align_bytes=64) for t in range(PACK)]
-        negmean = [sb.tile([P, 1], F32, name="negmean%d" % t) for t in range(PACK)]
-        zp = sb.tile([P, S // BLOCK, 2, BLOCK, 2], BF16, name="zp", align_bytes=64)
-        part = sb.tile([P, 1], F32, name="part")
-        nc.scalar.activation(out=hs[1][:, :HALF], in_=hb1_first[:], func=COPY, scale=-1.0 / S, accum_out=part[:])
+        h_scaled = [sb.tile([P, S], F32, name="h_scaled%d" % t, align_bytes=64) for t in range(PACK)]
+        minus_mean = [sb.tile([P, 1], F32, name="minus_mean%d" % t) for t in range(PACK)]
+        z_pairs = sb.tile([P, BLOCKS, 2, BLOCK, 2], BF16, name="z_pairs", align_bytes=64)
+        first_half_sum = sb.tile([P, 1], F32, name="first_half_sum")
+        nc.scalar.activation(out=h_scaled[SPLIT_TILE][:, :HALF], in_=h_split_first[:], func=COPY, scale=-1.0 / S, accum_out=first_half_sum[:])
         for t in range(PACK):
-            if t == 1:
-                nc.vector.tensor_scalar(out=hs[t][:, HALF:], in0=hb[t][:, HALF:], scalar1=-1.0 / S, scalar2=part[:], op0=MULT, op1=ADD, accum_out=negmean[t][:])
+            if t == SPLIT_TILE:
+                nc.vector.tensor_scalar(out=h_scaled[t][:, HALF:], in0=h_bank[t][:, HALF:], scalar1=-1.0 / S, scalar2=first_half_sum[:], op0=MULT, op1=ADD, accum_out=minus_mean[t][:])
             else:
-                nc.scalar.activation(out=hs[t][:], in_=hb[t][:], func=COPY, scale=-1.0 / S, accum_out=negmean[t][:])
-        def centre(t, lo, hi):
-            nc.vector.tensor_scalar(out=zp[:, lo:hi, t // 2, :, t % 2], in0=hs[t][:].rearrange("p (b c) -> p b c", c=BLOCK)[:, lo:hi],
-                                    scalar1=-float(S), scalar2=negmean[t][:], op0=MULT, op1=ADD)
+                nc.scalar.activation(out=h_scaled[t][:], in_=h_bank[t][:], func=COPY, scale=-1.0 / S, accum_out=minus_mean[t][:])
 
-        for t in range(PACK - 1):
-            centre(t, 0, 4)
-        for lo, hi in ((0, 1), (1, 2), (2, 4)):
-            centre(3, lo, hi)
+        def centre(t, first_block, end_block):
+            nc.vector.tensor_scalar(
+                out=z_pairs[:, first_block:end_block, t // 2, :, t % 2],
+                in0=h_scaled[t][:].rearrange("p (b c) -> p b c", c=BLOCK)[:, first_block:end_block],
+                scalar1=-float(S),
+                scalar2=minus_mean[t][:],
+                op0=MULT,
+                op1=ADD,
+            )
 
-        zwords = zp[:].rearrange("p b u c e -> p b u (c e)").bitcast(F32)
-        banks = ["ob0", "ob1", "ob2", "hb1_first", "hb0", "hb1", "hb2", "hb3"]
-        out_v = out.rearrange("(a p) j -> p a j", p=P)
-        zg = []
-        for b in range(S // BLOCK):
-            cols = slice(b * BLOCK, (b + 1) * BLOCK)
-            zg.append(sb.tile([P, BLOCK * PACK], BF16, name="zg%d" % b, align_bytes=64))
-            zsrc = zwords[:, b].rearrange("p u c -> p c u")
-            zdst = zg[b][:].bitcast(F32).rearrange("p (c u) -> p c u", u=2)
-            if b in (0, 1):
-                nc.scalar.copy(out=zdst, in_=zsrc)
+        last = PACK - 1
+        for t in range(last):
+            centre(t, 0, BLOCKS)
+        centre(last, 0, 1)
+        centre(last, 1, 2)
+        centre(last, 2, BLOCKS)
+
+        pair_words = z_pairs[:].rearrange("p b v c e -> p b v (c e)").bitcast(F32)
+        z_bf = []
+        for b in range(BLOCKS):
+            z_bf.append(sb.tile([P, BLOCK * PACK], BF16, name="z_bf%d" % b, align_bytes=64))
+            weave_in = pair_words[:, b].rearrange("p v c -> p c v")
+            weave_out = z_bf[b][:].bitcast(F32).rearrange("p (c v) -> p c v", v=2)
+            if b < SCALAR_WEAVES:
+                nc.scalar.copy(out=weave_out, in_=weave_in)
             else:
-                nc.vector.tensor_copy(out=zdst, in_=zsrc)
-        for b in range(S // BLOCK):
-            cols = slice(b * BLOCK, (b + 1) * BLOCK)
-            zq = sb.tile([P, BLOCK], U32, name="zq%d" % b, align_bytes=64)
-            zs = sb.tile([P, BLOCK], U8, name="zs%d" % b, align_bytes=64)
-            nc.vector.quantize_mx(out=zq[:].bitcast(FP8X4), scales=zs[:], in_=zg[b][:])
-            res = sb.tile([P, 2, BLOCK], F32, name="res%d" % b, align_bytes=64)
-            for a in range(2):
-                mc = slice(a * P, (a + 1) * P)
-                ob = ps.tile([P, BLOCK], F32, name="ob%d%d" % (b, a), tag=banks[2 * b + a])
-                nc.tensor.matmul_mx(out=ob[:], lhsT=w2w[:, mc].bitcast(FP8X4), lhsT_scale=w2s[:, mc],
-                                    rhs=zq[:].bitcast(FP8X4), rhs_scale=zs[:], start=True, stop=True)
+                nc.vector.tensor_copy(out=weave_out, in_=weave_in)
+
+        out_banks = ["fresh0", "fresh1", "fresh2", "h_split_first"] + ["h_bank%d" % t for t in range(PACK)]
+        out_rows = out.rearrange("(a p) j -> p a j", p=P)
+        for b in range(BLOCKS):
+            z_codes = sb.tile([P, BLOCK], U32, name="z_codes%d" % b, align_bytes=64)
+            z_scales = sb.tile([P, BLOCK], U8, name="z_scales%d" % b, align_bytes=64)
+            nc.vector.quantize_mx(out=z_codes[:].bitcast(FP8X4), scales=z_scales[:], in_=z_bf[b][:])
+            result = sb.tile([P, OUT_TILES, BLOCK], F32, name="result%d" % b, align_bytes=64)
+            for a in range(OUT_TILES):
+                rows = slice(a * P, (a + 1) * P)
+                acc = ps.tile([P, BLOCK], F32, name="acc%d%d" % (b, a), tag=out_banks[OUT_TILES * b + a])
+                nc.tensor.matmul_mx(
+                    out=acc[:],
+                    lhsT=w2w[:, rows].bitcast(FP8X4),
+                    lhsT_scale=w2s[:, rows],
+                    rhs=z_codes[:].bitcast(FP8X4),
+                    rhs_scale=z_scales[:],
+                    start=True,
+                    stop=True,
+                )
                 if a == 0 or b == 0:
-                    nc.scalar.copy(out=res[:, a], in_=ob[:])
+                    nc.scalar.copy(out=result[:, a], in_=acc[:])
                 else:
-                    nc.vector.tensor_copy(out=res[:, a], in_=ob[:])
-            nc.sync.dma_start(out=out_v[:, :, cols], in_=res[:])
+                    nc.vector.tensor_copy(out=result[:, a], in_=acc[:])
+            nc.sync.dma_start(out=out_rows[:, :, b * BLOCK : (b + 1) * BLOCK], in_=result[:])

@@ -24,6 +24,7 @@ HALF = S // 2
 BLOCK = 128
 BLOCKS = S // BLOCK
 OUT_TILES = N // P
+WARM_ROWS = 64
 SPLIT_TILE = 1
 SCALAR_WEAVES = 3
 
@@ -78,8 +79,26 @@ def tile_picked_deepset_none_p_kernel(tc, x_words, x_scales, w1, w2_words, w2_sc
         h_bank = [ps.tile([P, S], F32, name="h_bank%d" % t) for t in range(PACK)]
         h_split_first = ps.tile([P, HALF], F32, name="h_split_first")
 
-        def quantise_w1(v):
-            nc.vector.quantize_mx(out=w1_codes[v][:].bitcast(FP8X4), scales=w1_scales[v][:], in_=w1_bf[v][:].rearrange("p e m r -> p (e m r)"))
+        z_codes = sb.tile([P, S], U32, name="z_codes", align_bytes=64)
+        nc.vector.memset(z_codes[:].bitcast(I32), 0)
+        warm_bank = ps.tile([WARM_ROWS, S], F32, name="warm_bank", tag="fresh0")
+        for warm_pass in range(2):
+            nc.tensor.matmul_mx(
+                out=warm_bank[:],
+                lhsT=z_codes[:, :WARM_ROWS].bitcast(FP8X4),
+                lhsT_scale=picked_scales[:, :WARM_ROWS],
+                rhs=z_codes[:].bitcast(FP8X4),
+                rhs_scale=picked_scales[:],
+                start=True,
+                stop=True,
+            )
+
+        def quantise_w1(v, first, end):
+            nc.vector.quantize_mx(
+                out=w1_codes[v][:, first * P : end * P].bitcast(FP8X4),
+                scales=w1_scales[v][:, first * P : end * P],
+                in_=w1_bf[v][:, first:end].rearrange("p e m r -> p (e m r)"),
+            )
 
         def gather_words(lo, hi):
             nc.vector.tensor_copy(picked_words[:, lo:hi], xw[:].bitcast(U32).indirect(offsets[:, lo // LIST_ROWS : hi // LIST_ROWS]))
@@ -96,14 +115,15 @@ def tile_picked_deepset_none_p_kernel(tc, x_words, x_scales, w1, w2_words, w2_sc
                 stop=True,
             )
 
-        quantise_w1(0)
-        for lo in (0, HALF):
+        quantise_w1(0, 0, 2)
+        for lo, tiles in ((0, (SPLIT_TILE, 0)), (HALF, (0, SPLIT_TILE))):
             gather_words(lo, lo + HALF)
-            first_product(0, lo, lo + HALF)
-            first_product(1, lo, lo + HALF)
+            for t in tiles:
+                first_product(t, lo, lo + HALF)
         w1_codes.append(sb.tile([P, 2 * P], U32, name="w1_codes1", tag="window", align_bytes=64))
-        quantise_w1(1)
+        quantise_w1(1, 0, 1)
         first_product(2, 0, S)
+        quantise_w1(1, 1, 2)
         first_product(3, 0, S)
 
         h_scaled = [sb.tile([P, S], F32, name="h_scaled%d" % t, align_bytes=64) for t in range(PACK)]
@@ -148,9 +168,9 @@ def tile_picked_deepset_none_p_kernel(tc, x_words, x_scales, w1, w2_words, w2_sc
         out_banks = ["fresh0", "fresh1", "fresh2", "h_split_first"] + ["h_bank%d" % t for t in range(PACK)]
         out_rows = out.rearrange("(a p) j -> p a j", p=P)
         for b in range(BLOCKS):
-            z_codes = sb.tile([P, BLOCK], U32, name="z_codes%d" % b, align_bytes=64)
+            block_codes = z_codes[:, b * BLOCK : (b + 1) * BLOCK].bitcast(FP8X4)
             z_scales = sb.tile([P, BLOCK], U8, name="z_scales%d" % b, align_bytes=64)
-            nc.vector.quantize_mx(out=z_codes[:].bitcast(FP8X4), scales=z_scales[:], in_=z_bf[b][:])
+            nc.vector.quantize_mx(out=block_codes, scales=z_scales[:], in_=z_bf[b][:])
             result = sb.tile([P, OUT_TILES, BLOCK], F32, name="result%d" % b, align_bytes=64)
             for a in range(OUT_TILES):
                 rows = slice(a * P, (a + 1) * P)
@@ -159,7 +179,7 @@ def tile_picked_deepset_none_p_kernel(tc, x_words, x_scales, w1, w2_words, w2_sc
                     out=acc[:],
                     lhsT=w2w[:, rows].bitcast(FP8X4),
                     lhsT_scale=w2s[:, rows],
-                    rhs=z_codes[:].bitcast(FP8X4),
+                    rhs=block_codes,
                     rhs_scale=z_scales[:],
                     start=True,
                     stop=True,

@@ -25,8 +25,7 @@ BLOCK = 128
 BLOCKS = S // BLOCK
 OUT_TILES = N // P
 WARM_ROWS = 64
-SPLIT_TILE = 1
-SCALAR_WEAVES = 3
+SCALAR_WEAVES = (0, 3)
 
 
 def tile_picked_deepset_none_p_kernel(tc, x_words, x_scales, w1, w2_words, w2_scales, offs, out):
@@ -76,8 +75,8 @@ def tile_picked_deepset_none_p_kernel(tc, x_words, x_scales, w1, w2_words, w2_sc
         w1_codes = [sb.tile([P, 2 * P], U32, name="w1_codes0", align_bytes=64)]
         w1_scales = [sb.tile([P, 2 * P], U8, name="w1_scales%d" % v, align_bytes=64) for v in range(2)]
         picked_words = sb.tile([P, S], U32, name="picked_words", align_bytes=64)
-        h_bank = [ps.tile([P, S], F32, name="h_bank%d" % t) for t in range(PACK)]
-        h_split_first = ps.tile([P, HALF], F32, name="h_split_first")
+        h_half = [[ps.tile([P, HALF], F32, name="h_half%d%d" % (t, half)) for half in range(2)] for t in range(2)]
+        h_whole = [ps.tile([P, S], F32, name="h_whole%d" % t) for t in range(2, PACK)]
 
         z_codes = sb.tile([P, S], U32, name="z_codes", align_bytes=64)
         nc.vector.memset(z_codes[:].bitcast(I32), 0)
@@ -105,21 +104,22 @@ def tile_picked_deepset_none_p_kernel(tc, x_words, x_scales, w1, w2_words, w2_sc
 
         def first_product(t, lo, hi):
             channels = slice((t % 2) * P, (t % 2 + 1) * P)
-            nc.tensor.matmul_mx(
-                out=h_split_first[:] if (t, hi) == (SPLIT_TILE, HALF) else h_bank[t][:, lo:hi],
-                lhsT=w1_codes[t // 2][:, channels].bitcast(FP8X4),
-                lhsT_scale=w1_scales[t // 2][:, channels],
-                rhs=picked_words[:, lo:hi].bitcast(FP8X4),
-                rhs_scale=picked_scales[:, lo:hi],
-                start=True,
-                stop=True,
-            )
+            for c in range(lo, hi, BLOCK):
+                nc.tensor.matmul_mx(
+                    out=h_half[t][c // HALF][:, c % HALF : c % HALF + BLOCK] if t < 2 else h_whole[t - 2][:, c : c + BLOCK],
+                    lhsT=w1_codes[t // 2][:, channels].bitcast(FP8X4),
+                    lhsT_scale=w1_scales[t // 2][:, channels],
+                    rhs=picked_words[:, c : c + BLOCK].bitcast(FP8X4),
+                    rhs_scale=picked_scales[:, c : c + BLOCK],
+                    start=True,
+                    stop=True,
+                )
 
         quantise_w1(0, 0, 2)
-        for lo, tiles in ((0, (SPLIT_TILE, 0)), (HALF, (0, SPLIT_TILE))):
+        for lo in (0, HALF):
             gather_words(lo, lo + HALF)
-            for t in tiles:
-                first_product(t, lo, lo + HALF)
+            first_product(0, lo, lo + HALF)
+            first_product(1, lo, lo + HALF)
         w1_codes.append(sb.tile([P, 2 * P], U32, name="w1_codes1", tag="window", align_bytes=64))
         quantise_w1(1, 0, 1)
         first_product(2, 0, S)
@@ -129,13 +129,18 @@ def tile_picked_deepset_none_p_kernel(tc, x_words, x_scales, w1, w2_words, w2_sc
         h_scaled = [sb.tile([P, S], F32, name="h_scaled%d" % t, align_bytes=64) for t in range(PACK)]
         minus_mean = [sb.tile([P, 1], F32, name="minus_mean%d" % t) for t in range(PACK)]
         z_pairs = sb.tile([P, BLOCKS, 2, BLOCK, 2], BF16, name="z_pairs", align_bytes=64)
-        first_half_sum = sb.tile([P, 1], F32, name="first_half_sum")
-        nc.scalar.activation(out=h_scaled[SPLIT_TILE][:, :HALF], in_=h_split_first[:], func=COPY, scale=-1.0 / S, accum_out=first_half_sum[:])
-        for t in range(PACK):
-            if t == SPLIT_TILE:
-                nc.vector.tensor_scalar(out=h_scaled[t][:, HALF:], in0=h_bank[t][:, HALF:], scalar1=-1.0 / S, scalar2=first_half_sum[:], op0=MULT, op1=ADD, accum_out=minus_mean[t][:])
-            else:
-                nc.scalar.activation(out=h_scaled[t][:], in_=h_bank[t][:], func=COPY, scale=-1.0 / S, accum_out=minus_mean[t][:])
+        part_sum = [sb.tile([P, 1], F32, name="part_sum%d" % i) for i in range(3)]
+
+        def scalar_sum(t, bank, lo, hi, total):
+            nc.scalar.activation(out=h_scaled[t][:, lo:hi], in_=bank[:], func=COPY, scale=-1.0 / S, accum_out=total[:])
+
+        scalar_sum(0, h_half[0][0], 0, HALF, part_sum[0])
+        scalar_sum(1, h_half[1][0], 0, HALF, part_sum[1])
+        scalar_sum(1, h_half[1][1], HALF, S, part_sum[2])
+        nc.vector.tensor_scalar(out=h_scaled[0][:, HALF:], in0=h_half[0][1][:], scalar1=-1.0 / S, scalar2=part_sum[0][:], op0=MULT, op1=ADD, accum_out=minus_mean[0][:])
+        nc.vector.tensor_tensor(out=minus_mean[1][:], in0=part_sum[1][:], in1=part_sum[2][:], op=ADD)
+        for t in range(2, PACK):
+            scalar_sum(t, h_whole[t - 2], 0, S, minus_mean[t])
 
         def centre(t, first_block, end_block):
             nc.vector.tensor_scalar(
@@ -160,12 +165,12 @@ def tile_picked_deepset_none_p_kernel(tc, x_words, x_scales, w1, w2_words, w2_sc
             z_bf.append(sb.tile([P, BLOCK * PACK], BF16, name="z_bf%d" % b, align_bytes=64))
             weave_in = pair_words[:, b].rearrange("p v c -> p c v")
             weave_out = z_bf[b][:].bitcast(F32).rearrange("p (c v) -> p c v", v=2)
-            if b < SCALAR_WEAVES:
+            if b in SCALAR_WEAVES:
                 nc.scalar.copy(out=weave_out, in_=weave_in)
             else:
                 nc.vector.tensor_copy(out=weave_out, in_=weave_in)
 
-        out_banks = ["fresh0", "fresh1", "fresh2", "h_split_first"] + ["h_bank%d" % t for t in range(PACK)]
+        out_banks = ["fresh0", "fresh1", "h_half00", "h_half10", "h_half01", "h_half11", "h_whole2", "h_whole3"]
         out_rows = out.rearrange("(a p) j -> p a j", p=P)
         for b in range(BLOCKS):
             block_codes = z_codes[:, b * BLOCK : (b + 1) * BLOCK].bitcast(FP8X4)
@@ -184,7 +189,7 @@ def tile_picked_deepset_none_p_kernel(tc, x_words, x_scales, w1, w2_words, w2_sc
                     start=True,
                     stop=True,
                 )
-                if a == 0 or b == 0:
+                if a == 0:
                     nc.scalar.copy(out=result[:, a], in_=acc[:])
                 else:
                     nc.vector.tensor_copy(out=result[:, a], in_=acc[:])

@@ -25,7 +25,7 @@ BLOCK = 128
 BLOCKS = S // BLOCK
 OUT_TILES = N // P
 WARM_ROWS = 64
-SCALAR_WEAVES = (0, 3)
+SCALAR_WEAVES = (1, 3)
 
 
 def tile_picked_deepset_none_p_kernel(tc, x_words, x_scales, w1, w2_words, w2_scales, offs, out):
@@ -128,7 +128,7 @@ def tile_picked_deepset_none_p_kernel(tc, x_words, x_scales, w1, w2_words, w2_sc
 
         h_scaled = [sb.tile([P, S], F32, name="h_scaled%d" % t, align_bytes=64) for t in range(PACK)]
         minus_mean = [sb.tile([P, 1], F32, name="minus_mean%d" % t) for t in range(PACK)]
-        z_pairs = sb.tile([P, BLOCKS, 2, BLOCK, 2], BF16, name="z_pairs", align_bytes=64)
+        z_pairs = sb.tile([P, 2 * BLOCKS, 2, BLOCK // 2, 2], BF16, name="z_pairs", align_bytes=64)
         part_sum = [sb.tile([P, 1], F32, name="part_sum%d" % i) for i in range(3)]
 
         def scalar_sum(t, bank, lo, hi, total):
@@ -144,8 +144,20 @@ def tile_picked_deepset_none_p_kernel(tc, x_words, x_scales, w1, w2_words, w2_sc
 
         def centre(t, first_block, end_block):
             nc.vector.tensor_scalar(
-                out=z_pairs[:, first_block:end_block, t // 2, :, t % 2],
-                in0=h_scaled[t][:].rearrange("p (b c) -> p b c", c=BLOCK)[:, first_block:end_block],
+                out=z_pairs[:, 2 * first_block : 2 * end_block, t // 2, :, t % 2],
+                in0=h_scaled[t][:].rearrange("p (b c) -> p b c", c=BLOCK // 2)[:, 2 * first_block : 2 * end_block],
+                scalar1=-float(S),
+                scalar2=minus_mean[t][:],
+                op0=MULT,
+                op1=ADD,
+            )
+
+        z_bf = [sb.tile([P, BLOCK * PACK], BF16, name="z_bf%d" % b, align_bytes=64) for b in range(BLOCKS)]
+
+        def centre_first(t):
+            nc.vector.tensor_scalar(
+                out=z_bf[0][:].rearrange("p (c r) -> p c r", r=PACK)[:, :, t],
+                in0=h_scaled[t][:, :BLOCK],
                 scalar1=-float(S),
                 scalar2=minus_mean[t][:],
                 op0=MULT,
@@ -154,21 +166,24 @@ def tile_picked_deepset_none_p_kernel(tc, x_words, x_scales, w1, w2_words, w2_sc
 
         last = PACK - 1
         for t in range(last):
-            centre(t, 0, BLOCKS)
-        centre(last, 0, 1)
+            centre_first(t)
+            centre(t, 1, BLOCKS)
         centre(last, 1, 2)
+        centre_first(last)
         centre(last, 2, BLOCKS)
 
         pair_words = z_pairs[:].rearrange("p b v c e -> p b v (c e)").bitcast(F32)
-        z_bf = []
-        for b in range(BLOCKS):
-            z_bf.append(sb.tile([P, BLOCK * PACK], BF16, name="z_bf%d" % b, align_bytes=64))
-            weave_in = pair_words[:, b].rearrange("p v c -> p c v")
-            weave_out = z_bf[b][:].bitcast(F32).rearrange("p (c v) -> p c v", v=2)
+
+        def weave(b):
+            weave_in = pair_words[:, 2 * b : 2 * b + 2].rearrange("p u v c -> p u c v")
+            weave_out = z_bf[b][:].bitcast(F32).rearrange("p (u c v) -> p u c v", u=2, v=2)
             if b in SCALAR_WEAVES:
                 nc.scalar.copy(out=weave_out, in_=weave_in)
             else:
                 nc.vector.tensor_copy(out=weave_out, in_=weave_in)
+
+        weave(1)
+        weave(3)
 
         out_banks = ["fresh0", "fresh1", "h_half00", "h_half10", "h_half01", "h_half11", "h_whole2", "h_whole3"]
         out_rows = out.rearrange("(a p) j -> p a j", p=P)
@@ -176,6 +191,8 @@ def tile_picked_deepset_none_p_kernel(tc, x_words, x_scales, w1, w2_words, w2_sc
             block_codes = z_codes[:, b * BLOCK : (b + 1) * BLOCK].bitcast(FP8X4)
             z_scales = sb.tile([P, BLOCK], U8, name="z_scales%d" % b, align_bytes=64)
             nc.vector.quantize_mx(out=block_codes, scales=z_scales[:], in_=z_bf[b][:])
+            if b == 0:
+                weave(2)
             result = sb.tile([P, OUT_TILES, BLOCK], F32, name="result%d" % b, align_bytes=64)
             for a in range(OUT_TILES):
                 rows = slice(a * P, (a + 1) * P)
@@ -189,7 +206,7 @@ def tile_picked_deepset_none_p_kernel(tc, x_words, x_scales, w1, w2_words, w2_sc
                     start=True,
                     stop=True,
                 )
-                if a == 0:
+                if a == 0 or b < 2:
                     nc.scalar.copy(out=result[:, a], in_=acc[:])
                 else:
                     nc.vector.tensor_copy(out=result[:, a], in_=acc[:])

@@ -15,6 +15,7 @@ FP8X4 = mybir.dt.float8_e4m3fn_x4
 MULT = mybir.AluOpType.mult
 ADD = mybir.AluOpType.add
 COPY = mybir.ActivationFunctionType.Copy
+IDENTITY = mybir.ActivationFunctionType.Identity
 
 P = 128
 PACK = 4
@@ -25,7 +26,9 @@ BLOCK = 128
 BLOCKS = S // BLOCK
 OUT_TILES = N // P
 WARM_ROWS = 64
-SCALAR_WEAVES = (1, 3)
+SCALAR_CENTRES = 128
+DIRECT = 1
+SCALAR_EMPTIES = 1
 
 
 def tile_picked_deepset_none_p_kernel(tc, x_words, x_scales, w1, w2_words, w2_scales, offs, out):
@@ -128,71 +131,61 @@ def tile_picked_deepset_none_p_kernel(tc, x_words, x_scales, w1, w2_words, w2_sc
 
         h_scaled = [sb.tile([P, S], F32, name="h_scaled%d" % t, align_bytes=64) for t in range(PACK)]
         minus_mean = [sb.tile([P, 1], F32, name="minus_mean%d" % t) for t in range(PACK)]
-        z_pairs = sb.tile([P, 2 * BLOCKS, 2, BLOCK // 2, 2], BF16, name="z_pairs", align_bytes=64)
+        z_pairs = sb.tile([P, 2, S - BLOCK, 2], BF16, name="z_pairs", align_bytes=64)
         part_sum = [sb.tile([P, 1], F32, name="part_sum%d" % i) for i in range(3)]
 
         def scalar_sum(t, bank, lo, hi, total):
             nc.scalar.activation(out=h_scaled[t][:, lo:hi], in_=bank[:], func=COPY, scale=-1.0 / S, accum_out=total[:])
 
         scalar_sum(0, h_half[0][0], 0, HALF, part_sum[0])
-        scalar_sum(1, h_half[1][0], 0, HALF, part_sum[1])
+        nc.vector.tensor_scalar(out=h_scaled[1][:, :HALF], in0=h_half[1][0][:], scalar1=-1.0 / S, scalar2=0.0, op0=MULT, op1=ADD, accum_out=part_sum[1][:])
         scalar_sum(1, h_half[1][1], HALF, S, part_sum[2])
         nc.vector.tensor_scalar(out=h_scaled[0][:, HALF:], in0=h_half[0][1][:], scalar1=-1.0 / S, scalar2=part_sum[0][:], op0=MULT, op1=ADD, accum_out=minus_mean[0][:])
         nc.vector.tensor_tensor(out=minus_mean[1][:], in0=part_sum[1][:], in1=part_sum[2][:], op=ADD)
         for t in range(2, PACK):
             scalar_sum(t, h_whole[t - 2], 0, S, minus_mean[t])
 
-        def centre(t, first_block, end_block):
+        def centre(t, lo, hi):
             nc.vector.tensor_scalar(
-                out=z_pairs[:, 2 * first_block : 2 * end_block, t // 2, :, t % 2],
-                in0=h_scaled[t][:].rearrange("p (b c) -> p b c", c=BLOCK // 2)[:, 2 * first_block : 2 * end_block],
+                out=z_pairs[:, t // 2, lo - BLOCK : hi - BLOCK, t % 2],
+                in0=h_scaled[t][:, lo:hi],
                 scalar1=-float(S),
                 scalar2=minus_mean[t][:],
                 op0=MULT,
                 op1=ADD,
             )
 
-        z_bf = [sb.tile([P, BLOCK * PACK], BF16, name="z_bf%d" % b, align_bytes=64) for b in range(BLOCKS)]
-
-        def centre_first(t):
-            nc.vector.tensor_scalar(
-                out=z_bf[0][:].rearrange("p (c r) -> p c r", r=PACK)[:, :, t],
-                in0=h_scaled[t][:, :BLOCK],
-                scalar1=-float(S),
-                scalar2=minus_mean[t][:],
-                op0=MULT,
-                op1=ADD,
+        def centre_on_scalar(t, lo, hi):
+            nc.scalar.activation(
+                out=z_pairs[:, t // 2, lo - BLOCK : hi - BLOCK, t % 2], in_=h_scaled[t][:, lo:hi], func=IDENTITY, scale=-float(S), bias=minus_mean[t][:]
             )
 
-        last = PACK - 1
-        for t in range(last):
-            centre_first(t)
-            centre(t, 1, BLOCKS)
-        centre(last, 1, 2)
-        centre_first(last)
-        centre(last, 2, BLOCKS)
+        z_direct = sb.tile([P, DIRECT * BLOCK * PACK], BF16, name="z_direct", align_bytes=64)
+        z_bf = [z_direct[:, b * BLOCK * PACK : (b + 1) * BLOCK * PACK] for b in range(DIRECT)]
+        z_bf.extend(sb.tile([P, BLOCK * PACK], BF16, name="z_bf%d" % b, align_bytes=64)[:] for b in range(DIRECT, BLOCKS))
 
-        pair_words = z_pairs[:].rearrange("p b v c e -> p b v (c e)").bitcast(F32)
+        def centre_direct(t, first_block, end_block):
+            entries = slice(first_block * BLOCK, end_block * BLOCK)
+            nc.vector.tensor_scalar(out=z_direct[:].rearrange("p (c r) -> p c r", r=PACK)[:, entries, t], in0=h_scaled[t][:, entries], scalar1=-float(S), scalar2=minus_mean[t][:], op0=MULT, op1=ADD)
 
-        def weave(b):
-            weave_in = pair_words[:, 2 * b : 2 * b + 2].rearrange("p u v c -> p u c v")
-            weave_out = z_bf[b][:].bitcast(F32).rearrange("p (u c v) -> p u c v", u=2, v=2)
-            if b in SCALAR_WEAVES:
-                nc.scalar.copy(out=weave_out, in_=weave_in)
-            else:
-                nc.vector.tensor_copy(out=weave_out, in_=weave_in)
+        pair_words = z_pairs[:].rearrange("p v c e -> p v (c e)").bitcast(F32)
 
-        weave(1)
-        weave(3)
+        def weave(b, copy):
+            copy(
+                out=z_bf[b].bitcast(F32).rearrange("p (c v) -> p c v", v=2),
+                in_=pair_words[:, :, (b - 1) * BLOCK : b * BLOCK].rearrange("p v c -> p c v"),
+            )
 
         out_banks = ["fresh0", "fresh1", "h_half00", "h_half10", "h_half01", "h_half11", "h_whole2", "h_whole3"]
         out_rows = out.rearrange("(a p) j -> p a j", p=P)
-        for b in range(BLOCKS):
-            block_codes = z_codes[:, b * BLOCK : (b + 1) * BLOCK].bitcast(FP8X4)
-            z_scales = sb.tile([P, BLOCK], U8, name="z_scales%d" % b, align_bytes=64)
-            nc.vector.quantize_mx(out=block_codes, scales=z_scales[:], in_=z_bf[b][:])
-            if b == 0:
-                weave(2)
+        z_scales = [sb.tile([P, BLOCK], U8, name="z_scales%d" % b, align_bytes=64) for b in range(BLOCKS)]
+
+        def quantise_z(b):
+            entries = slice(b * BLOCK, (b + 1) * BLOCK)
+            nc.vector.quantize_mx(out=z_codes[:, entries].bitcast(FP8X4), scales=z_scales[b][:], in_=z_bf[b])
+
+        def second_product(b):
+            entries = slice(b * BLOCK, (b + 1) * BLOCK)
             result = sb.tile([P, OUT_TILES, BLOCK], F32, name="result%d" % b, align_bytes=64)
             for a in range(OUT_TILES):
                 rows = slice(a * P, (a + 1) * P)
@@ -201,13 +194,35 @@ def tile_picked_deepset_none_p_kernel(tc, x_words, x_scales, w1, w2_words, w2_sc
                     out=acc[:],
                     lhsT=w2w[:, rows].bitcast(FP8X4),
                     lhsT_scale=w2s[:, rows],
-                    rhs=block_codes,
-                    rhs_scale=z_scales[:],
+                    rhs=z_codes[:, entries].bitcast(FP8X4),
+                    rhs_scale=z_scales[b][:],
                     start=True,
                     stop=True,
                 )
-                if a == 0 or b < 2:
+                if a == 0 or b < SCALAR_EMPTIES:
                     nc.scalar.copy(out=result[:, a], in_=acc[:])
                 else:
                     nc.vector.tensor_copy(out=result[:, a], in_=acc[:])
-            nc.sync.dma_start(out=out_rows[:, :, b * BLOCK : (b + 1) * BLOCK], in_=result[:])
+                if b in (0, BLOCKS - 1):
+                    nc.sync.dma_start(out=out_rows[:, a, entries], in_=result[:, a])
+            if b not in (0, BLOCKS - 1):
+                nc.sync.dma_start(out=out_rows[:, :, entries], in_=result[:])
+
+        last = PACK - 1
+        for t in range(2):
+            centre_direct(t, 0, DIRECT)
+            centre(t, BLOCK, S - SCALAR_CENTRES)
+            centre_on_scalar(t, S - SCALAR_CENTRES, S)
+        centre_direct(2, 0, DIRECT)
+        centre(2, BLOCK, S)
+        centre(last, BLOCK, 2 * BLOCK)
+        centre_direct(last, 0, 1)
+        centre(last, 2 * BLOCK, S)
+        weave(1, nc.scalar.copy)
+        weave(3, nc.scalar.copy)
+        quantise_z(0)
+        weave(2, nc.vector.tensor_copy)
+        for b in range(1, BLOCKS):
+            quantise_z(b)
+        for b in range(BLOCKS):
+            second_product(b)

@@ -25,7 +25,6 @@ HALF = S // 2
 BLOCK = 128
 BLOCKS = S // BLOCK
 OUT_TILES = N // P
-WARM_ROWS = 64
 SCALAR_CENTRES = 128
 DIRECT = 1
 SCALAR_EMPTIES = 1
@@ -82,18 +81,6 @@ def tile_picked_deepset_none_p_kernel(tc, x_words, x_scales, w1, w2_words, w2_sc
         h_whole = [ps.tile([P, S], F32, name="h_whole%d" % t) for t in range(2, PACK)]
 
         z_codes = sb.tile([P, S], U32, name="z_codes", align_bytes=64)
-        nc.vector.memset(z_codes[:].bitcast(I32), 0)
-        warm_bank = ps.tile([WARM_ROWS, S], F32, name="warm_bank", tag="fresh0")
-        for warm_pass in range(2):
-            nc.tensor.matmul_mx(
-                out=warm_bank[:],
-                lhsT=z_codes[:, :WARM_ROWS].bitcast(FP8X4),
-                lhsT_scale=picked_scales[:, :WARM_ROWS],
-                rhs=z_codes[:].bitcast(FP8X4),
-                rhs_scale=picked_scales[:],
-                start=True,
-                stop=True,
-            )
 
         def quantise_w1(v, first, end):
             nc.vector.quantize_mx(
@@ -119,6 +106,17 @@ def tile_picked_deepset_none_p_kernel(tc, x_words, x_scales, w1, w2_words, w2_sc
                 )
 
         quantise_w1(0, 0, 2)
+        warm_bank = ps.tile([P, 2 * P], F32, name="warm_bank", tag="fresh0")
+        for warm_pass in range(2):
+            nc.tensor.matmul_mx(
+                out=warm_bank[:],
+                lhsT=w1_codes[0][:, :P].bitcast(FP8X4),
+                lhsT_scale=w1_scales[0][:, :P],
+                rhs=w1_codes[0][:].bitcast(FP8X4),
+                rhs_scale=w1_scales[0][:],
+                start=True,
+                stop=True,
+            )
         for lo in (0, HALF):
             gather_words(lo, lo + HALF)
             first_product(0, lo, lo + HALF)

@@ -28,6 +28,7 @@ OUT_TILES = N // P
 SCALAR_CENTRES = 128
 DIRECT = 1
 SCALAR_EMPTIES = 1
+STORE_FROM = {0: 0, 1: 1, 3: 2}
 
 
 def tile_picked_deepset_none_p_kernel(tc, x_words, x_scales, w1, w2_words, w2_scales, offs, out):
@@ -178,13 +179,14 @@ def tile_picked_deepset_none_p_kernel(tc, x_words, x_scales, w1, w2_words, w2_sc
         out_rows = out.rearrange("(a p) j -> p a j", p=P)
         z_scales = [sb.tile([P, BLOCK], U8, name="z_scales%d" % b, align_bytes=64) for b in range(BLOCKS)]
 
+        result = [sb.tile([P, S], F32, name="result%d" % a, align_bytes=64) for a in range(OUT_TILES)]
+
         def quantise_z(b):
             entries = slice(b * BLOCK, (b + 1) * BLOCK)
             nc.vector.quantize_mx(out=z_codes[:, entries].bitcast(FP8X4), scales=z_scales[b][:], in_=z_bf[b])
 
         def second_product(b):
             entries = slice(b * BLOCK, (b + 1) * BLOCK)
-            result = sb.tile([P, OUT_TILES, BLOCK], F32, name="result%d" % b, align_bytes=64)
             for a in range(OUT_TILES):
                 rows = slice(a * P, (a + 1) * P)
                 acc = ps.tile([P, BLOCK], F32, name="acc%d%d" % (b, a), tag=out_banks[OUT_TILES * b + a])
@@ -198,13 +200,12 @@ def tile_picked_deepset_none_p_kernel(tc, x_words, x_scales, w1, w2_words, w2_sc
                     stop=True,
                 )
                 if a == 0 or b < SCALAR_EMPTIES:
-                    nc.scalar.copy(out=result[:, a], in_=acc[:])
+                    nc.scalar.copy(out=result[a][:, entries], in_=acc[:])
                 else:
-                    nc.vector.tensor_copy(out=result[:, a], in_=acc[:])
-                if b in (0, BLOCKS - 1):
-                    nc.sync.dma_start(out=out_rows[:, a, entries], in_=result[:, a])
-            if b not in (0, BLOCKS - 1):
-                nc.sync.dma_start(out=out_rows[:, :, entries], in_=result[:])
+                    nc.vector.tensor_copy(out=result[a][:, entries], in_=acc[:])
+                if b in STORE_FROM:
+                    stored = slice(STORE_FROM[b] * BLOCK, (b + 1) * BLOCK)
+                    nc.sync.dma_start(out=out_rows[:, a, stored], in_=result[a][:, stored])
 
         last = PACK - 1
         for t in range(2):

@@ -25,9 +25,12 @@ HALF = S // 2
 BLOCK = 128
 BLOCKS = S // BLOCK
 OUT_TILES = N // P
+WARM_ROWS = 64
 SCALAR_CENTRES = 128
 DIRECT = 1
 SCALAR_EMPTIES = 1
+EARLY_VECTOR_CAST = 88
+VECTOR_CASTS = (80, 48)
 STORE_FROM = {0: 0, 1: 1, 3: 2}
 
 
@@ -39,45 +42,63 @@ def tile_picked_deepset_none_p_kernel(tc, x_words, x_scales, w1, w2_words, w2_sc
 
         offsets = sb.tile([P, S // LIST_ROWS], U16, name="offsets")
         w1_raw = [sb.tile([P, 2, H], F32, name="w1_raw%d" % u, align_bytes=64) for u in range(2)]
-        xw = sb.tile([P, T], I32, name="xw", tag="window", align_bytes=64)
+        xw = sb.tile([P, T], I32, name="xw", align_bytes=64)
         xs = sb.tile([P, T], U8, name="xs", align_bytes=64)
         w2w = sb.tile([P, N], I32, name="w2w", align_bytes=64)
         w2s = sb.tile([P, N], U8, name="w2s", align_bytes=64)
 
         nc.vector.memset(xs[:].bitcast(I32), 0)
         nc.vector.memset(w2s[:].bitcast(I32), 0)
-        warm_in = sb.tile([P, 1], F32, name="warm_in")
-        warm_out = sb.tile([P, 1], F32, name="warm_out")
-        nc.gpsimd.memset(warm_in[:], 0.0)
-        nc.scalar.activation(out=warm_out[:], in_=warm_in[:], func=COPY, scale=-1.0 / S)
 
         def load_scale_rows(tile, rows):
             for q in range(QUADRANTS):
                 nc.sync.dma_start(out=tile[32 * q : 32 * q + 4, :].bitcast(I32), in_=rows[4 * q : 4 * q + 4, :].bitcast(I32))
 
         w1_rows = w1.rearrange("(p r) i -> p r i", r=PACK)
-        nc.sync.dma_start(out=w1_raw[0][:], in_=w1_rows[:, 0:2])
+        x_rows = x_words[0].rearrange("p c r -> p (c r)").bitcast(I32)
+        nc.sync.dma_start(out=xw[:, : T // 2], in_=x_rows[:, : T // 2])
         nc.sync.dma_start(offsets[:], offs)
         load_scale_rows(xs, x_scales[0])
-        nc.sync.dma_start(out=w1_raw[1][:], in_=w1_rows[:, 2:4])
-        nc.sync.dma_start(out=xw[:], in_=x_words[0].rearrange("p c r -> p (c r)").bitcast(I32))
+        nc.sync.dma_start(out=xw[:, T // 2 :], in_=x_rows[:, T // 2 :])
+        for u in range(2):
+            nc.sync.dma_start(out=w1_raw[u][:], in_=w1_rows[:, 2 * u : 2 * u + 2])
         nc.sync.dma_start(out=w2w[:], in_=w2_words[0].rearrange("p c r -> p (c r)").bitcast(I32))
         load_scale_rows(w2s, w2_scales[0])
 
         picked_scales = sb.tile([P, S], U8, name="picked_scales", align_bytes=64)
         nc.vector.tensor_copy(picked_scales[:], xs[:].indirect(offsets[:]))
+        picked_words = sb.tile([P, S], U32, name="picked_words", align_bytes=64)
+        nc.vector.tensor_copy(picked_words[:], xw[:].bitcast(U32).indirect(offsets[:]))
+
+        warm_bank = ps.tile([WARM_ROWS, S], F32, name="warm_bank", tag="fresh0")
+        for warm_pass in range(2):
+            nc.tensor.matmul_mx(
+                out=warm_bank[:],
+                lhsT=picked_words[:, :WARM_ROWS].bitcast(FP8X4),
+                lhsT_scale=picked_scales[:, :WARM_ROWS],
+                rhs=picked_words[:].bitcast(FP8X4),
+                rhs_scale=picked_scales[:],
+                start=True,
+                stop=True,
+            )
+
 
         w1_bf = [sb.tile([P, 2, P, PACK], BF16, name="w1_bf%d" % v, align_bytes=64) for v in range(2)]
         cast_in = [w1_raw[u][:].rearrange("p r (m t) -> p m r t", t=PACK) for u in range(2)]
         cast_out = [w1_bf[v][:].rearrange("p e m r -> p m r e") for v in range(2)]
-        nc.scalar.copy(out=cast_out[0][:, :, 0:2], in_=cast_in[0][:, :, :, 0:2])
-        nc.scalar.copy(out=cast_out[1][:, :, 0:2], in_=cast_in[0][:, :, :, 2:4])
-        nc.vector.tensor_copy(out=cast_out[0][:, :, 2:4], in_=cast_in[1][:, :, :, 0:2])
-        nc.scalar.copy(out=cast_out[1][:, :, 2:4], in_=cast_in[1][:, :, :, 2:4])
 
-        w1_codes = [sb.tile([P, 2 * P], U32, name="w1_codes0", align_bytes=64)]
+        def cast_w1(u, v, first, end, copy):
+            copy(out=cast_out[v][:, first:end, 2 * u : 2 * u + 2], in_=cast_in[u][:, first:end, :, 2 * v : 2 * v + 2])
+
+        cast_w1(0, 0, 0, P, nc.scalar.copy)
+        cast_w1(0, 1, 0, EARLY_VECTOR_CAST, nc.vector.tensor_copy)
+        cast_w1(0, 1, EARLY_VECTOR_CAST, P, nc.scalar.copy)
+        for v in range(2):
+            cast_w1(1, v, 0, VECTOR_CASTS[v], nc.vector.tensor_copy)
+            cast_w1(1, v, VECTOR_CASTS[v], P, nc.scalar.copy)
+
+        w1_codes = [sb.tile([P, 2 * P], U32, name="w1_codes%d" % v, align_bytes=64) for v in range(2)]
         w1_scales = [sb.tile([P, 2 * P], U8, name="w1_scales%d" % v, align_bytes=64) for v in range(2)]
-        picked_words = sb.tile([P, S], U32, name="picked_words", align_bytes=64)
         h_half = [[ps.tile([P, HALF], F32, name="h_half%d%d" % (t, half)) for half in range(2)] for t in range(2)]
         h_whole = [ps.tile([P, S], F32, name="h_whole%d" % t) for t in range(2, PACK)]
 
@@ -90,43 +111,23 @@ def tile_picked_deepset_none_p_kernel(tc, x_words, x_scales, w1, w2_words, w2_sc
                 in_=w1_bf[v][:, first:end].rearrange("p e m r -> p (e m r)"),
             )
 
-        def gather_words(lo, hi):
-            nc.vector.tensor_copy(picked_words[:, lo:hi], xw[:].bitcast(U32).indirect(offsets[:, lo // LIST_ROWS : hi // LIST_ROWS]))
-
         def first_product(t, lo, hi):
             channels = slice((t % 2) * P, (t % 2 + 1) * P)
-            for c in range(lo, hi, BLOCK):
+            width = BLOCK if t < 2 else HALF
+            for c in range(lo, hi, width):
                 nc.tensor.matmul_mx(
-                    out=h_half[t][c // HALF][:, c % HALF : c % HALF + BLOCK] if t < 2 else h_whole[t - 2][:, c : c + BLOCK],
+                    out=h_half[t][c // HALF][:, c % HALF : c % HALF + width] if t < 2 else h_whole[t - 2][:, c : c + width],
                     lhsT=w1_codes[t // 2][:, channels].bitcast(FP8X4),
                     lhsT_scale=w1_scales[t // 2][:, channels],
-                    rhs=picked_words[:, c : c + BLOCK].bitcast(FP8X4),
-                    rhs_scale=picked_scales[:, c : c + BLOCK],
+                    rhs=picked_words[:, c : c + width].bitcast(FP8X4),
+                    rhs_scale=picked_scales[:, c : c + width],
                     start=True,
                     stop=True,
                 )
 
-        quantise_w1(0, 0, 2)
-        warm_bank = ps.tile([P, 2 * P], F32, name="warm_bank", tag="fresh0")
-        for warm_pass in range(2):
-            nc.tensor.matmul_mx(
-                out=warm_bank[:],
-                lhsT=w1_codes[0][:, :P].bitcast(FP8X4),
-                lhsT_scale=w1_scales[0][:, :P],
-                rhs=w1_codes[0][:].bitcast(FP8X4),
-                rhs_scale=w1_scales[0][:],
-                start=True,
-                stop=True,
-            )
-        for lo in (0, HALF):
-            gather_words(lo, lo + HALF)
-            first_product(0, lo, lo + HALF)
-            first_product(1, lo, lo + HALF)
-        w1_codes.append(sb.tile([P, 2 * P], U32, name="w1_codes1", tag="window", align_bytes=64))
-        quantise_w1(1, 0, 1)
-        first_product(2, 0, S)
-        quantise_w1(1, 1, 2)
-        first_product(3, 0, S)
+        for t in range(PACK):
+            quantise_w1(t // 2, t % 2, t % 2 + 1)
+            first_product(t, 0, S)
 
         h_scaled = [sb.tile([P, S], F32, name="h_scaled%d" % t, align_bytes=64) for t in range(PACK)]
         minus_mean = [sb.tile([P, 1], F32, name="minus_mean%d" % t) for t in range(PACK)]
@@ -137,9 +138,9 @@ def tile_picked_deepset_none_p_kernel(tc, x_words, x_scales, w1, w2_words, w2_sc
             nc.scalar.activation(out=h_scaled[t][:, lo:hi], in_=bank[:], func=COPY, scale=-1.0 / S, accum_out=total[:])
 
         scalar_sum(0, h_half[0][0], 0, HALF, part_sum[0])
-        nc.vector.tensor_scalar(out=h_scaled[1][:, :HALF], in0=h_half[1][0][:], scalar1=-1.0 / S, scalar2=0.0, op0=MULT, op1=ADD, accum_out=part_sum[1][:])
-        scalar_sum(1, h_half[1][1], HALF, S, part_sum[2])
         nc.vector.tensor_scalar(out=h_scaled[0][:, HALF:], in0=h_half[0][1][:], scalar1=-1.0 / S, scalar2=part_sum[0][:], op0=MULT, op1=ADD, accum_out=minus_mean[0][:])
+        scalar_sum(1, h_half[1][0], 0, HALF, part_sum[1])
+        scalar_sum(1, h_half[1][1], HALF, S, part_sum[2])
         nc.vector.tensor_tensor(out=minus_mean[1][:], in0=part_sum[1][:], in1=part_sum[2][:], op=ADD)
         for t in range(2, PACK):
             scalar_sum(t, h_whole[t - 2], 0, S, minus_mean[t])

@@ -26,11 +26,11 @@ BLOCK = 128
 BLOCKS = S // BLOCK
 OUT_TILES = N // P
 WARM_ROWS = 64
+WARM_PASSES = 1
 SCALAR_CENTRES = 128
 DIRECT = 1
 SCALAR_EMPTIES = 1
-EARLY_VECTOR_CAST = 88
-VECTOR_CASTS = (80, 48)
+LATE_SCALAR_CAST = 40
 STORE_FROM = {0: 0, 1: 1, 3: 2}
 
 
@@ -41,7 +41,7 @@ def tile_picked_deepset_none_p_kernel(tc, x_words, x_scales, w1, w2_words, w2_sc
         ps = ctx.enter_context(tc.psum_pool(name="ps", bufs=1))
 
         offsets = sb.tile([P, S // LIST_ROWS], U16, name="offsets")
-        w1_raw = [sb.tile([P, 2, H], F32, name="w1_raw%d" % u, align_bytes=64) for u in range(2)]
+        w1_raw = [[sb.tile([P, 2, H // 2], F32, name="w1_raw%d%d" % (u, side), align_bytes=64) for side in range(2)] for u in range(2)]
         xw = sb.tile([P, T], I32, name="xw", align_bytes=64)
         xs = sb.tile([P, T], U8, name="xs", align_bytes=64)
         w2w = sb.tile([P, N], I32, name="w2w", align_bytes=64)
@@ -56,12 +56,17 @@ def tile_picked_deepset_none_p_kernel(tc, x_words, x_scales, w1, w2_words, w2_sc
 
         w1_rows = w1.rearrange("(p r) i -> p r i", r=PACK)
         x_rows = x_words[0].rearrange("p c r -> p (c r)").bitcast(I32)
-        nc.sync.dma_start(out=xw[:, : T // 2], in_=x_rows[:, : T // 2])
+
+        def load_w1(u, side):
+            nc.sync.dma_start(out=w1_raw[u][side][:], in_=w1_rows[:, 2 * u : 2 * u + 2, side * H // 2 : (side + 1) * H // 2])
+
+        load_w1(0, 0)
         nc.sync.dma_start(offsets[:], offs)
         load_scale_rows(xs, x_scales[0])
-        nc.sync.dma_start(out=xw[:, T // 2 :], in_=x_rows[:, T // 2 :])
-        for u in range(2):
-            nc.sync.dma_start(out=w1_raw[u][:], in_=w1_rows[:, 2 * u : 2 * u + 2])
+        nc.sync.dma_start(out=xw[:], in_=x_rows)
+        load_w1(0, 1)
+        load_w1(1, 0)
+        load_w1(1, 1)
         nc.sync.dma_start(out=w2w[:], in_=w2_words[0].rearrange("p c r -> p (c r)").bitcast(I32))
         load_scale_rows(w2s, w2_scales[0])
 
@@ -71,7 +76,7 @@ def tile_picked_deepset_none_p_kernel(tc, x_words, x_scales, w1, w2_words, w2_sc
         nc.vector.tensor_copy(picked_words[:], xw[:].bitcast(U32).indirect(offsets[:]))
 
         warm_bank = ps.tile([WARM_ROWS, S], F32, name="warm_bank", tag="fresh0")
-        for warm_pass in range(2):
+        for warm_pass in range(WARM_PASSES):
             nc.tensor.matmul_mx(
                 out=warm_bank[:],
                 lhsT=picked_words[:, :WARM_ROWS].bitcast(FP8X4),
@@ -84,18 +89,21 @@ def tile_picked_deepset_none_p_kernel(tc, x_words, x_scales, w1, w2_words, w2_sc
 
 
         w1_bf = [sb.tile([P, 2, P, PACK], BF16, name="w1_bf%d" % v, align_bytes=64) for v in range(2)]
-        cast_in = [w1_raw[u][:].rearrange("p r (m t) -> p m r t", t=PACK) for u in range(2)]
+        cast_in = [[w1_raw[u][side][:].rearrange("p r (m t) -> p m r t", t=PACK) for side in range(2)] for u in range(2)]
         cast_out = [w1_bf[v][:].rearrange("p e m r -> p m r e") for v in range(2)]
 
-        def cast_w1(u, v, first, end, copy):
-            copy(out=cast_out[v][:, first:end, 2 * u : 2 * u + 2], in_=cast_in[u][:, first:end, :, 2 * v : 2 * v + 2])
+        def cast_w1(u, side, v, first, end, copy):
+            base = side * P // 2
+            copy(out=cast_out[v][:, base + first : base + end, 2 * u : 2 * u + 2], in_=cast_in[u][side][:, first:end, :, 2 * v : 2 * v + 2])
 
-        cast_w1(0, 0, 0, P, nc.scalar.copy)
-        cast_w1(0, 1, 0, EARLY_VECTOR_CAST, nc.vector.tensor_copy)
-        cast_w1(0, 1, EARLY_VECTOR_CAST, P, nc.scalar.copy)
+        for side in range(2):
+            for v in range(2):
+                cast_w1(0, side, v, 0, P // 2, nc.scalar.copy)
         for v in range(2):
-            cast_w1(1, v, 0, VECTOR_CASTS[v], nc.vector.tensor_copy)
-            cast_w1(1, v, VECTOR_CASTS[v], P, nc.scalar.copy)
+            cast_w1(1, 0, v, 0, P // 2, nc.vector.tensor_copy)
+        cast_w1(1, 1, 0, 0, LATE_SCALAR_CAST, nc.scalar.copy)
+        cast_w1(1, 1, 0, LATE_SCALAR_CAST, P // 2, nc.vector.tensor_copy)
+        cast_w1(1, 1, 1, 0, P // 2, nc.vector.tensor_copy)
 
         w1_codes = [sb.tile([P, 2 * P], U32, name="w1_codes%d" % v, align_bytes=64) for v in range(2)]
         w1_scales = [sb.tile([P, 2 * P], U8, name="w1_scales%d" % v, align_bytes=64) for v in range(2)]

@@ -26,7 +26,7 @@ BLOCK = 128
 BLOCKS = S // BLOCK
 OUT_TILES = N // P
 WARM_ROWS = 64
-WARM_PASSES = 1
+WARM_PASSES = 2
 SCALAR_CENTRES = 128
 DIRECT = 1
 SCALAR_EMPTIES = 1

@@ -30,7 +30,6 @@ WARM_PASSES = 2
 SCALAR_CENTRES = 128
 DIRECT = 1
 SCALAR_EMPTIES = 1
-LATE_SCALAR_CAST = 40
 STORE_FROM = {0: 0, 1: 1, 3: 2}
 
 
@@ -60,29 +59,32 @@ def tile_picked_deepset_none_p_kernel(tc, x_words, x_scales, w1, w2_words, w2_sc
         def load_w1(u, side):
             nc.sync.dma_start(out=w1_raw[u][side][:], in_=w1_rows[:, 2 * u : 2 * u + 2, side * H // 2 : (side + 1) * H // 2])
 
-        load_w1(0, 0)
-        nc.sync.dma_start(offsets[:], offs)
-        load_scale_rows(xs, x_scales[0])
         nc.sync.dma_start(out=xw[:], in_=x_rows)
+        nc.sync.dma_start(offsets[:], offs)
+        load_w1(0, 0)
+        load_scale_rows(xs, x_scales[0])
         load_w1(0, 1)
         load_w1(1, 0)
         load_w1(1, 1)
         nc.sync.dma_start(out=w2w[:], in_=w2_words[0].rearrange("p c r -> p (c r)").bitcast(I32))
         load_scale_rows(w2s, w2_scales[0])
 
-        picked_scales = sb.tile([P, S], U8, name="picked_scales", align_bytes=64)
-        nc.vector.tensor_copy(picked_scales[:], xs[:].indirect(offsets[:]))
         picked_words = sb.tile([P, S], U32, name="picked_words", align_bytes=64)
         nc.vector.tensor_copy(picked_words[:], xw[:].bitcast(U32).indirect(offsets[:]))
+        picked_scales = [sb.tile([P, HALF], U8, name="picked_scales%d" % half, align_bytes=64) for half in range(2)]
+        half_columns = HALF // LIST_ROWS
+        for half in range(2):
+            nc.vector.tensor_copy(picked_scales[half][:], xs[:].indirect(offsets[:, half * half_columns : (half + 1) * half_columns]))
+        word_bytes = picked_words[:].bitcast(U8)
 
         warm_bank = ps.tile([WARM_ROWS, S], F32, name="warm_bank", tag="fresh0")
         for warm_pass in range(WARM_PASSES):
             nc.tensor.matmul_mx(
                 out=warm_bank[:],
                 lhsT=picked_words[:, :WARM_ROWS].bitcast(FP8X4),
-                lhsT_scale=picked_scales[:, :WARM_ROWS],
+                lhsT_scale=picked_scales[0][:, :WARM_ROWS],
                 rhs=picked_words[:].bitcast(FP8X4),
-                rhs_scale=picked_scales[:],
+                rhs_scale=word_bytes[:, :S],
                 start=True,
                 stop=True,
             )
@@ -99,11 +101,10 @@ def tile_picked_deepset_none_p_kernel(tc, x_words, x_scales, w1, w2_words, w2_sc
         for side in range(2):
             for v in range(2):
                 cast_w1(0, side, v, 0, P // 2, nc.scalar.copy)
-        for v in range(2):
-            cast_w1(1, 0, v, 0, P // 2, nc.vector.tensor_copy)
-        cast_w1(1, 1, 0, 0, LATE_SCALAR_CAST, nc.scalar.copy)
-        cast_w1(1, 1, 0, LATE_SCALAR_CAST, P // 2, nc.vector.tensor_copy)
-        cast_w1(1, 1, 1, 0, P // 2, nc.vector.tensor_copy)
+        cast_w1(1, 0, 0, 0, P // 2, nc.vector.tensor_copy)
+        cast_w1(1, 1, 0, 0, P // 2, nc.vector.tensor_copy)
+        cast_w1(1, 0, 1, 0, P // 2, nc.vector.tensor_copy)
+        cast_w1(1, 1, 1, 0, P // 2, nc.scalar.copy)
 
         w1_codes = [sb.tile([P, 2 * P], U32, name="w1_codes%d" % v, align_bytes=64) for v in range(2)]
         w1_scales = [sb.tile([P, 2 * P], U8, name="w1_scales%d" % v, align_bytes=64) for v in range(2)]
@@ -128,7 +129,7 @@ def tile_picked_deepset_none_p_kernel(tc, x_words, x_scales, w1, w2_words, w2_sc
                     lhsT=w1_codes[t // 2][:, channels].bitcast(FP8X4),
                     lhsT_scale=w1_scales[t // 2][:, channels],
                     rhs=picked_words[:, c : c + width].bitcast(FP8X4),
-                    rhs_scale=picked_scales[:, c : c + width],
+                    rhs_scale=picked_scales[c // HALF][:, c % HALF : c % HALF + width],
                     start=True,
                     stop=True,
                 )

@@ -30,6 +30,7 @@ WARM_PASSES = 2
 SCALAR_CENTRES = 128
 DIRECT = 1
 SCALAR_EMPTIES = 1
+VECTOR_CASTS = (80, 56)
 STORE_FROM = {0: 0, 1: 1, 3: 2}
 
 
@@ -40,7 +41,8 @@ def tile_picked_deepset_none_p_kernel(tc, x_words, x_scales, w1, w2_words, w2_sc
         ps = ctx.enter_context(tc.psum_pool(name="ps", bufs=1))
 
         offsets = sb.tile([P, S // LIST_ROWS], U16, name="offsets")
-        w1_raw = [[sb.tile([P, 2, H // 2], F32, name="w1_raw%d%d" % (u, side), align_bytes=64) for side in range(2)] for u in range(2)]
+        w1_early = [sb.tile([P, 2, H // 2], F32, name="w1_early%d" % side, align_bytes=64) for side in range(2)]
+        w1_late = sb.tile([P, 2, H], F32, name="w1_late", align_bytes=64)
         xw = sb.tile([P, T], I32, name="xw", align_bytes=64)
         xs = sb.tile([P, T], U8, name="xs", align_bytes=64)
         w2w = sb.tile([P, N], I32, name="w2w", align_bytes=64)
@@ -56,25 +58,23 @@ def tile_picked_deepset_none_p_kernel(tc, x_words, x_scales, w1, w2_words, w2_sc
         w1_rows = w1.rearrange("(p r) i -> p r i", r=PACK)
         x_rows = x_words[0].rearrange("p c r -> p (c r)").bitcast(I32)
 
-        def load_w1(u, side):
-            nc.sync.dma_start(out=w1_raw[u][side][:], in_=w1_rows[:, 2 * u : 2 * u + 2, side * H // 2 : (side + 1) * H // 2])
+        def load_early(side):
+            nc.sync.dma_start(out=w1_early[side][:], in_=w1_rows[:, 0:2, side * H // 2 : (side + 1) * H // 2])
 
-        nc.sync.dma_start(out=xw[:], in_=x_rows)
         nc.sync.dma_start(offsets[:], offs)
-        load_w1(0, 0)
+        nc.sync.dma_start(out=xw[:], in_=x_rows)
+        load_early(0)
         load_scale_rows(xs, x_scales[0])
-        load_w1(0, 1)
-        load_w1(1, 0)
-        load_w1(1, 1)
+        load_early(1)
+        nc.sync.dma_start(out=w1_late[:], in_=w1_rows[:, 2:4])
         nc.sync.dma_start(out=w2w[:], in_=w2_words[0].rearrange("p c r -> p (c r)").bitcast(I32))
         load_scale_rows(w2s, w2_scales[0])
 
         picked_words = sb.tile([P, S], U32, name="picked_words", align_bytes=64)
         nc.vector.tensor_copy(picked_words[:], xw[:].bitcast(U32).indirect(offsets[:]))
-        picked_scales = [sb.tile([P, HALF], U8, name="picked_scales%d" % half, align_bytes=64) for half in range(2)]
-        half_columns = HALF // LIST_ROWS
-        for half in range(2):
-            nc.vector.tensor_copy(picked_scales[half][:], xs[:].indirect(offsets[:, half * half_columns : (half + 1) * half_columns]))
+        picked_scales = sb.tile([P, S], U8, name="picked_scales", align_bytes=64)
+        for lo, hi in ((0, BLOCK), (BLOCK, S)):
+            nc.vector.tensor_copy(picked_scales[:, lo:hi], xs[:].indirect(offsets[:, lo // LIST_ROWS : hi // LIST_ROWS]))
         word_bytes = picked_words[:].bitcast(U8)
 
         warm_bank = ps.tile([WARM_ROWS, S], F32, name="warm_bank", tag="fresh0")
@@ -82,7 +82,7 @@ def tile_picked_deepset_none_p_kernel(tc, x_words, x_scales, w1, w2_words, w2_sc
             nc.tensor.matmul_mx(
                 out=warm_bank[:],
                 lhsT=picked_words[:, :WARM_ROWS].bitcast(FP8X4),
-                lhsT_scale=picked_scales[0][:, :WARM_ROWS],
+                lhsT_scale=picked_scales[:, :WARM_ROWS],
                 rhs=picked_words[:].bitcast(FP8X4),
                 rhs_scale=word_bytes[:, :S],
                 start=True,
@@ -91,20 +91,22 @@ def tile_picked_deepset_none_p_kernel(tc, x_words, x_scales, w1, w2_words, w2_sc
 
 
         w1_bf = [sb.tile([P, 2, P, PACK], BF16, name="w1_bf%d" % v, align_bytes=64) for v in range(2)]
-        cast_in = [[w1_raw[u][side][:].rearrange("p r (m t) -> p m r t", t=PACK) for side in range(2)] for u in range(2)]
         cast_out = [w1_bf[v][:].rearrange("p e m r -> p m r e") for v in range(2)]
 
-        def cast_w1(u, side, v, first, end, copy):
-            base = side * P // 2
-            copy(out=cast_out[v][:, base + first : base + end, 2 * u : 2 * u + 2], in_=cast_in[u][side][:, first:end, :, 2 * v : 2 * v + 2])
+        def cast_early(side, v):
+            source = w1_early[side][:].rearrange("p r (m t) -> p m r t", t=PACK)
+            nc.scalar.copy(out=cast_out[v][:, side * P // 2 : (side + 1) * P // 2, 0:2], in_=source[:, :, :, 2 * v : 2 * v + 2])
+
+        def cast_late(v, first, end, copy):
+            source = w1_late[:].rearrange("p r (m t) -> p m r t", t=PACK)
+            copy(out=cast_out[v][:, first:end, 2:4], in_=source[:, first:end, :, 2 * v : 2 * v + 2])
 
         for side in range(2):
             for v in range(2):
-                cast_w1(0, side, v, 0, P // 2, nc.scalar.copy)
-        cast_w1(1, 0, 0, 0, P // 2, nc.vector.tensor_copy)
-        cast_w1(1, 1, 0, 0, P // 2, nc.vector.tensor_copy)
-        cast_w1(1, 0, 1, 0, P // 2, nc.vector.tensor_copy)
-        cast_w1(1, 1, 1, 0, P // 2, nc.scalar.copy)
+                cast_early(side, v)
+        for v in range(2):
+            cast_late(v, 0, VECTOR_CASTS[v], nc.vector.tensor_copy)
+            cast_late(v, VECTOR_CASTS[v], P, nc.scalar.copy)
 
         w1_codes = [sb.tile([P, 2 * P], U32, name="w1_codes%d" % v, align_bytes=64) for v in range(2)]
         w1_scales = [sb.tile([P, 2 * P], U8, name="w1_scales%d" % v, align_bytes=64) for v in range(2)]
@@ -129,7 +131,7 @@ def tile_picked_deepset_none_p_kernel(tc, x_words, x_scales, w1, w2_words, w2_sc
                     lhsT=w1_codes[t // 2][:, channels].bitcast(FP8X4),
                     lhsT_scale=w1_scales[t // 2][:, channels],
                     rhs=picked_words[:, c : c + width].bitcast(FP8X4),
-                    rhs_scale=picked_scales[c // HALF][:, c % HALF : c % HALF + width],
+                    rhs_scale=picked_scales[:, c : c + width],
                     start=True,
                     stop=True,
                 )

@@ -30,7 +30,6 @@ WARM_PASSES = 2
 SCALAR_CENTRES = 128
 DIRECT = 1
 SCALAR_EMPTIES = 1
-VECTOR_CASTS = (80, 56)
 STORE_FROM = {0: 0, 1: 1, 3: 2}
 
 
@@ -101,12 +100,17 @@ def tile_picked_deepset_none_p_kernel(tc, x_words, x_scales, w1, w2_words, w2_sc
             source = w1_late[:].rearrange("p r (m t) -> p m r t", t=PACK)
             copy(out=cast_out[v][:, first:end, 2:4], in_=source[:, first:end, :, 2 * v : 2 * v + 2])
 
+        def cast_late_tile(t, first, end, copy):
+            source = w1_late[:].rearrange("p r (m t) -> p m r t", t=PACK)
+            copy(out=cast_out[t // 2][:, first:end, 2:4, t % 2], in_=source[:, first:end, :, t])
+
         for side in range(2):
             for v in range(2):
                 cast_early(side, v)
-        for v in range(2):
-            cast_late(v, 0, VECTOR_CASTS[v], nc.vector.tensor_copy)
-            cast_late(v, VECTOR_CASTS[v], P, nc.scalar.copy)
+        cast_late_tile(0, 0, P // 2, nc.vector.tensor_copy)
+        cast_late_tile(0, P // 2, P, nc.scalar.copy)
+        cast_late_tile(1, 0, P, nc.vector.tensor_copy)
+        cast_late(1, 0, P, nc.scalar.copy)
 
         w1_codes = [sb.tile([P, 2 * P], U32, name="w1_codes%d" % v, align_bytes=64) for v in range(2)]
         w1_scales = [sb.tile([P, 2 * P], U8, name="w1_scales%d" % v, align_bytes=64) for v in range(2)]
@@ -143,7 +147,7 @@ def tile_picked_deepset_none_p_kernel(tc, x_words, x_scales, w1, w2_words, w2_sc
         h_scaled = [sb.tile([P, S], F32, name="h_scaled%d" % t, align_bytes=64) for t in range(PACK)]
         minus_mean = [sb.tile([P, 1], F32, name="minus_mean%d" % t) for t in range(PACK)]
         z_pairs = sb.tile([P, 2, S - BLOCK, 2], BF16, name="z_pairs", align_bytes=64)
-        part_sum = [sb.tile([P, 1], F32, name="part_sum%d" % i) for i in range(3)]
+        part_sum = [sb.tile([P, 1], F32, name="part_sum%d" % i) for i in range(2)]
 
         def scalar_sum(t, bank, lo, hi, total):
             nc.scalar.activation(out=h_scaled[t][:, lo:hi], in_=bank[:], func=COPY, scale=-1.0 / S, accum_out=total[:])
@@ -151,8 +155,7 @@ def tile_picked_deepset_none_p_kernel(tc, x_words, x_scales, w1, w2_words, w2_sc
         scalar_sum(0, h_half[0][0], 0, HALF, part_sum[0])
         nc.vector.tensor_scalar(out=h_scaled[0][:, HALF:], in0=h_half[0][1][:], scalar1=-1.0 / S, scalar2=part_sum[0][:], op0=MULT, op1=ADD, accum_out=minus_mean[0][:])
         scalar_sum(1, h_half[1][0], 0, HALF, part_sum[1])
-        scalar_sum(1, h_half[1][1], HALF, S, part_sum[2])
-        nc.vector.tensor_tensor(out=minus_mean[1][:], in0=part_sum[1][:], in1=part_sum[2][:], op=ADD)
+        nc.vector.tensor_scalar(out=h_scaled[1][:, HALF:], in0=h_half[1][1][:], scalar1=-1.0 / S, scalar2=part_sum[1][:], op0=MULT, op1=ADD, accum_out=minus_mean[1][:])
         for t in range(2, PACK):
             scalar_sum(t, h_whole[t - 2], 0, S, minus_mean[t])
 

@@ -21,14 +21,12 @@ P = 128
 PACK = 4
 QUADRANTS = 4
 LIST_ROWS = 16
-HALF = S // 2
 BLOCK = 128
 BLOCKS = S // BLOCK
 OUT_TILES = N // P
-WARM_ROWS = 64
+WARM_ROWS = 32
 WARM_PASSES = 2
-SCALAR_CENTRES = 128
-DIRECT = 1
+SCALAR_ENTRIES = 320
 SCALAR_EMPTIES = 1
 STORE_FROM = {0: 0, 1: 1, 3: 2}
 
@@ -88,7 +86,6 @@ def tile_picked_deepset_none_p_kernel(tc, x_words, x_scales, w1, w2_words, w2_sc
                 stop=True,
             )
 
-
         w1_bf = [sb.tile([P, 2, P, PACK], BF16, name="w1_bf%d" % v, align_bytes=64) for v in range(2)]
         cast_out = [w1_bf[v][:].rearrange("p e m r -> p m r e") for v in range(2)]
 
@@ -112,93 +109,56 @@ def tile_picked_deepset_none_p_kernel(tc, x_words, x_scales, w1, w2_words, w2_sc
         cast_late_tile(1, 0, P, nc.vector.tensor_copy)
         cast_late(1, 0, P, nc.scalar.copy)
 
-        w1_codes = [sb.tile([P, 2 * P], U32, name="w1_codes%d" % v, align_bytes=64) for v in range(2)]
-        w1_scales = [sb.tile([P, 2 * P], U8, name="w1_scales%d" % v, align_bytes=64) for v in range(2)]
-        h_half = [[ps.tile([P, HALF], F32, name="h_half%d%d" % (t, half)) for half in range(2)] for t in range(2)]
-        h_whole = [ps.tile([P, S], F32, name="h_whole%d" % t) for t in range(2, PACK)]
-
-        z_codes = sb.tile([P, S], U32, name="z_codes", align_bytes=64)
-
-        def quantise_w1(v, first, end):
-            nc.vector.quantize_mx(
-                out=w1_codes[v][:, first * P : end * P].bitcast(FP8X4),
-                scales=w1_scales[v][:, first * P : end * P],
-                in_=w1_bf[v][:, first:end].rearrange("p e m r -> p (e m r)"),
-            )
-
-        def first_product(t, lo, hi):
-            channels = slice((t % 2) * P, (t % 2 + 1) * P)
-            width = BLOCK if t < 2 else HALF
-            for c in range(lo, hi, width):
-                nc.tensor.matmul_mx(
-                    out=h_half[t][c // HALF][:, c % HALF : c % HALF + width] if t < 2 else h_whole[t - 2][:, c : c + width],
-                    lhsT=w1_codes[t // 2][:, channels].bitcast(FP8X4),
-                    lhsT_scale=w1_scales[t // 2][:, channels],
-                    rhs=picked_words[:, c : c + width].bitcast(FP8X4),
-                    rhs_scale=picked_scales[:, c : c + width],
-                    start=True,
-                    stop=True,
-                )
-
+        w1_codes = [sb.tile([P, P], U32, name="w1_codes%d" % t, align_bytes=64) for t in range(PACK)]
+        w1_scales = [sb.tile([P, P], U8, name="w1_scales%d" % t, align_bytes=64) for t in range(PACK)]
+        h_bank = [ps.tile([P, S], F32, name="h_bank%d" % t) for t in range(PACK)]
         for t in range(PACK):
-            quantise_w1(t // 2, t % 2, t % 2 + 1)
-            first_product(t, 0, S)
+            nc.vector.quantize_mx(out=w1_codes[t][:].bitcast(FP8X4), scales=w1_scales[t][:], in_=w1_bf[t // 2][:, t % 2].rearrange("p m r -> p (m r)"))
+            nc.tensor.matmul_mx(
+                out=h_bank[t][:],
+                lhsT=w1_codes[t][:].bitcast(FP8X4),
+                lhsT_scale=w1_scales[t][:],
+                rhs=picked_words[:].bitcast(FP8X4),
+                rhs_scale=picked_scales[:],
+                start=True,
+                stop=True,
+            )
 
         h_scaled = [sb.tile([P, S], F32, name="h_scaled%d" % t, align_bytes=64) for t in range(PACK)]
         minus_mean = [sb.tile([P, 1], F32, name="minus_mean%d" % t) for t in range(PACK)]
-        z_pairs = sb.tile([P, 2, S - BLOCK, 2], BF16, name="z_pairs", align_bytes=64)
-        part_sum = [sb.tile([P, 1], F32, name="part_sum%d" % i) for i in range(2)]
+        for t in range(PACK):
+            if t == 1:
+                nc.vector.tensor_scalar(out=h_scaled[t][:], in0=h_bank[t][:], scalar1=-1.0 / S, scalar2=None, op0=MULT, op1=ADD, accum_out=minus_mean[t][:])
+            else:
+                nc.scalar.activation(out=h_scaled[t][:], in_=h_bank[t][:], func=COPY, scale=-1.0 / S, accum_out=minus_mean[t][:])
 
-        def scalar_sum(t, bank, lo, hi, total):
-            nc.scalar.activation(out=h_scaled[t][:, lo:hi], in_=bank[:], func=COPY, scale=-1.0 / S, accum_out=total[:])
+        z_bf = [sb.tile([P, BLOCK, PACK], BF16, name="z_bf%d" % b, align_bytes=64) for b in range(BLOCKS)]
+        z_pairs = {b: sb.tile([P, 2, BLOCK, 2], BF16, name="z_pairs%d" % b, align_bytes=64) for b in range(1, BLOCKS)}
+        z_codes = [sb.tile([P, BLOCK], U32, name="z_codes%d" % b, align_bytes=64) for b in range(BLOCKS)]
+        z_scales = [sb.tile([P, BLOCK], U8, name="z_scales%d" % b, align_bytes=64) for b in range(BLOCKS)]
 
-        scalar_sum(0, h_half[0][0], 0, HALF, part_sum[0])
-        nc.vector.tensor_scalar(out=h_scaled[0][:, HALF:], in0=h_half[0][1][:], scalar1=-1.0 / S, scalar2=part_sum[0][:], op0=MULT, op1=ADD, accum_out=minus_mean[0][:])
-        scalar_sum(1, h_half[1][0], 0, HALF, part_sum[1])
-        nc.vector.tensor_scalar(out=h_scaled[1][:, HALF:], in0=h_half[1][1][:], scalar1=-1.0 / S, scalar2=part_sum[1][:], op0=MULT, op1=ADD, accum_out=minus_mean[1][:])
-        for t in range(2, PACK):
-            scalar_sum(t, h_whole[t - 2], 0, S, minus_mean[t])
+        def centre_vector(dst, t, lo, hi):
+            nc.vector.tensor_scalar(out=dst, in0=h_scaled[t][:, lo:hi], scalar1=-float(S), scalar2=minus_mean[t][:], op0=MULT, op1=ADD)
 
-        def centre(t, lo, hi):
-            nc.vector.tensor_scalar(
-                out=z_pairs[:, t // 2, lo - BLOCK : hi - BLOCK, t % 2],
-                in0=h_scaled[t][:, lo:hi],
-                scalar1=-float(S),
-                scalar2=minus_mean[t][:],
-                op0=MULT,
-                op1=ADD,
-            )
+        def centre_scalar(dst, t, lo, hi):
+            nc.scalar.activation(out=dst, in_=h_scaled[t][:, lo:hi], func=IDENTITY, scale=-float(S), bias=minus_mean[t][:])
 
-        def centre_on_scalar(t, lo, hi):
-            nc.scalar.activation(
-                out=z_pairs[:, t // 2, lo - BLOCK : hi - BLOCK, t % 2], in_=h_scaled[t][:, lo:hi], func=IDENTITY, scale=-float(S), bias=minus_mean[t][:]
-            )
-
-        z_direct = sb.tile([P, DIRECT * BLOCK * PACK], BF16, name="z_direct", align_bytes=64)
-        z_bf = [z_direct[:, b * BLOCK * PACK : (b + 1) * BLOCK * PACK] for b in range(DIRECT)]
-        z_bf.extend(sb.tile([P, BLOCK * PACK], BF16, name="z_bf%d" % b, align_bytes=64)[:] for b in range(DIRECT, BLOCKS))
-
-        def centre_direct(t, first_block, end_block):
-            entries = slice(first_block * BLOCK, end_block * BLOCK)
-            nc.vector.tensor_scalar(out=z_direct[:].rearrange("p (c r) -> p c r", r=PACK)[:, entries, t], in0=h_scaled[t][:, entries], scalar1=-float(S), scalar2=minus_mean[t][:], op0=MULT, op1=ADD)
-
-        pair_words = z_pairs[:].rearrange("p v c e -> p v (c e)").bitcast(F32)
+        def centre_pairs(centre, t, lo, hi):
+            b = lo // BLOCK
+            centre(z_pairs[b][:, t // 2, lo - b * BLOCK : hi - b * BLOCK, t % 2], t, lo, hi)
 
         def weave(b, copy):
             copy(
-                out=z_bf[b].bitcast(F32).rearrange("p (c v) -> p c v", v=2),
-                in_=pair_words[:, :, (b - 1) * BLOCK : b * BLOCK].rearrange("p v c -> p c v"),
+                out=z_bf[b][:].rearrange("p c r -> p (c r)").bitcast(F32).rearrange("p (c v) -> p c v", v=2),
+                in_=z_pairs[b][:].rearrange("p v c e -> p v (c e)").bitcast(F32).rearrange("p v c -> p c v"),
             )
 
-        out_banks = ["fresh0", "fresh1", "h_half00", "h_half10", "h_half01", "h_half11", "h_whole2", "h_whole3"]
-        out_rows = out.rearrange("(a p) j -> p a j", p=P)
-        z_scales = [sb.tile([P, BLOCK], U8, name="z_scales%d" % b, align_bytes=64) for b in range(BLOCKS)]
-
-        result = [sb.tile([P, S], F32, name="result%d" % a, align_bytes=64) for a in range(OUT_TILES)]
-
         def quantise_z(b):
-            entries = slice(b * BLOCK, (b + 1) * BLOCK)
-            nc.vector.quantize_mx(out=z_codes[:, entries].bitcast(FP8X4), scales=z_scales[b][:], in_=z_bf[b])
+            nc.vector.quantize_mx(out=z_codes[b][:].bitcast(FP8X4), scales=z_scales[b][:], in_=z_bf[b][:].rearrange("p c r -> p (c r)"))
+
+        out_banks = ["fresh0", "fresh1", "fresh2", "fresh3", "h_bank0", "h_bank1", "h_bank2", "h_bank3"]
+        out_rows = out.rearrange("(a p) j -> p a j", p=P)
+        result = [sb.tile([P, S], F32, name="result%d" % a, align_bytes=64) for a in range(OUT_TILES)]
 
         def second_product(b):
             entries = slice(b * BLOCK, (b + 1) * BLOCK)
@@ -209,7 +169,7 @@ def tile_picked_deepset_none_p_kernel(tc, x_words, x_scales, w1, w2_words, w2_sc
                     out=acc[:],
                     lhsT=w2w[:, rows].bitcast(FP8X4),
                     lhsT_scale=w2s[:, rows],
-                    rhs=z_codes[:, entries].bitcast(FP8X4),
+                    rhs=z_codes[b][:].bitcast(FP8X4),
                     rhs_scale=z_scales[b][:],
                     start=True,
                     stop=True,
@@ -222,21 +182,21 @@ def tile_picked_deepset_none_p_kernel(tc, x_words, x_scales, w1, w2_words, w2_sc
                     stored = slice(STORE_FROM[b] * BLOCK, (b + 1) * BLOCK)
                     nc.sync.dma_start(out=out_rows[:, a, stored], in_=result[a][:, stored])
 
-        last = PACK - 1
-        for t in range(2):
-            centre_direct(t, 0, DIRECT)
-            centre(t, BLOCK, S - SCALAR_CENTRES)
-            centre_on_scalar(t, S - SCALAR_CENTRES, S)
-        centre_direct(2, 0, DIRECT)
-        centre(2, BLOCK, S)
-        centre(last, BLOCK, 2 * BLOCK)
-        centre_direct(last, 0, 1)
-        centre(last, 2 * BLOCK, S)
-        weave(1, nc.scalar.copy)
-        weave(3, nc.scalar.copy)
+        border = BLOCK + SCALAR_ENTRIES
+        for t in range(PACK):
+            centre_vector(z_bf[0][:, :, t], t, 0, BLOCK)
         quantise_z(0)
-        weave(2, nc.vector.tensor_copy)
         for b in range(1, BLOCKS):
+            lo, hi = b * BLOCK, (b + 1) * BLOCK
+            for t in range(2):
+                if lo < border:
+                    centre_pairs(centre_scalar, t, lo, min(hi, border))
+                if hi > border:
+                    centre_pairs(centre_vector, t, max(lo, border), hi)
+            for t in range(2, PACK):
+                centre_pairs(centre_vector, t, lo, hi)
+        for b in range(1, BLOCKS):
+            weave(b, nc.scalar.copy if b == 2 else nc.vector.tensor_copy)
             quantise_z(b)
         for b in range(BLOCKS):
             second_product(b)

@@ -39,7 +39,7 @@ def tile_picked_deepset_none_p_kernel(tc, x_words, x_scales, w1, w2_words, w2_sc
 
         offsets = sb.tile([P, S // LIST_ROWS], U16, name="offsets")
         w1_early = [sb.tile([P, 2, H // 2], F32, name="w1_early%d" % side, align_bytes=64) for side in range(2)]
-        w1_late = sb.tile([P, 2, H], F32, name="w1_late", align_bytes=64)
+        w1_late = [sb.tile([P, 2, H // 2], F32, name="w1_late%d" % side, align_bytes=64) for side in range(2)]
         xw = sb.tile([P, T], I32, name="xw", align_bytes=64)
         xs = sb.tile([P, T], U8, name="xs", align_bytes=64)
         w2w = sb.tile([P, N], I32, name="w2w", align_bytes=64)
@@ -63,7 +63,8 @@ def tile_picked_deepset_none_p_kernel(tc, x_words, x_scales, w1, w2_words, w2_sc
         load_early(0)
         load_scale_rows(xs, x_scales[0])
         load_early(1)
-        nc.sync.dma_start(out=w1_late[:], in_=w1_rows[:, 2:4])
+        for side in range(2):
+            nc.sync.dma_start(out=w1_late[side][:], in_=w1_rows[:, 2:4, side * H // 2 : (side + 1) * H // 2])
         nc.sync.dma_start(out=w2w[:], in_=w2_words[0].rearrange("p c r -> p (c r)").bitcast(I32))
         load_scale_rows(w2s, w2_scales[0])
 
@@ -93,21 +94,19 @@ def tile_picked_deepset_none_p_kernel(tc, x_words, x_scales, w1, w2_words, w2_sc
             source = w1_early[side][:].rearrange("p r (m t) -> p m r t", t=PACK)
             nc.scalar.copy(out=cast_out[v][:, side * P // 2 : (side + 1) * P // 2, 0:2], in_=source[:, :, :, 2 * v : 2 * v + 2])
 
-        def cast_late(v, first, end, copy):
-            source = w1_late[:].rearrange("p r (m t) -> p m r t", t=PACK)
-            copy(out=cast_out[v][:, first:end, 2:4], in_=source[:, first:end, :, 2 * v : 2 * v + 2])
-
-        def cast_late_tile(t, first, end, copy):
-            source = w1_late[:].rearrange("p r (m t) -> p m r t", t=PACK)
-            copy(out=cast_out[t // 2][:, first:end, 2:4, t % 2], in_=source[:, first:end, :, t])
+        def cast_late(side, v, copy):
+            source = w1_late[side][:].rearrange("p r (m t) -> p m r t", t=PACK)
+            copy(out=cast_out[v][:, side * P // 2 : (side + 1) * P // 2, 2:4], in_=source[:, :, :, 2 * v : 2 * v + 2])
 
         for side in range(2):
             for v in range(2):
                 cast_early(side, v)
-        cast_late_tile(0, 0, P // 2, nc.vector.tensor_copy)
-        cast_late_tile(0, P // 2, P, nc.scalar.copy)
-        cast_late_tile(1, 0, P, nc.vector.tensor_copy)
-        cast_late(1, 0, P, nc.scalar.copy)
+        cast_late(0, 0, nc.vector.tensor_copy)
+        cast_late(0, 1, nc.scalar.copy)
+        last_quarter = w1_late[1][:].rearrange("p r (m t) -> p m r t", t=PACK)
+        for t in range(2):
+            nc.vector.tensor_copy(out=cast_out[0][:, P // 2 :, 2:4, t], in_=last_quarter[:, :, :, t])
+        cast_late(1, 1, nc.scalar.copy)
 
         w1_codes = [sb.tile([P, P], U32, name="w1_codes%d" % t, align_bytes=64) for t in range(PACK)]
         w1_scales = [sb.tile([P, P], U8, name="w1_scales%d" % t, align_bytes=64) for t in range(PACK)]

@@ -25,7 +25,7 @@ BLOCK = 128
 BLOCKS = S // BLOCK
 OUT_TILES = N // P
 WARM_ROWS = 32
-WARM_PASSES = 2
+WARM_COLUMNS = (512, 512, 128)
 SCALAR_ENTRIES = 320
 SCALAR_EMPTIES = 1
 STORE_FROM = {0: 0, 1: 1, 3: 2}
@@ -71,18 +71,17 @@ def tile_picked_deepset_none_p_kernel(tc, x_words, x_scales, w1, w2_words, w2_sc
         picked_words = sb.tile([P, S], U32, name="picked_words", align_bytes=64)
         nc.vector.tensor_copy(picked_words[:], xw[:].bitcast(U32).indirect(offsets[:]))
         picked_scales = sb.tile([P, S], U8, name="picked_scales", align_bytes=64)
-        for lo, hi in ((0, BLOCK), (BLOCK, S)):
-            nc.vector.tensor_copy(picked_scales[:, lo:hi], xs[:].indirect(offsets[:, lo // LIST_ROWS : hi // LIST_ROWS]))
+        nc.vector.tensor_copy(picked_scales[:], xs[:].indirect(offsets[:]))
         word_bytes = picked_words[:].bitcast(U8)
 
         warm_bank = ps.tile([WARM_ROWS, S], F32, name="warm_bank", tag="fresh0")
-        for warm_pass in range(WARM_PASSES):
+        for columns in WARM_COLUMNS:
             nc.tensor.matmul_mx(
-                out=warm_bank[:],
+                out=warm_bank[:, :columns],
                 lhsT=picked_words[:, :WARM_ROWS].bitcast(FP8X4),
-                lhsT_scale=picked_scales[:, :WARM_ROWS],
-                rhs=picked_words[:].bitcast(FP8X4),
-                rhs_scale=word_bytes[:, :S],
+                lhsT_scale=word_bytes[:, :WARM_ROWS],
+                rhs=picked_words[:, :columns].bitcast(FP8X4),
+                rhs_scale=word_bytes[:, :columns],
                 start=True,
                 stop=True,
             )

@@ -181,19 +181,18 @@ def tile_picked_deepset_none_p_kernel(tc, x_words, x_scales, w1, w2_words, w2_sc
                     nc.sync.dma_start(out=out_rows[:, a, stored], in_=result[a][:, stored])
 
         border = BLOCK + SCALAR_ENTRIES
+        for lo in range(BLOCK, border, BLOCK):
+            for t in range(2):
+                centre_pairs(centre_scalar, t, lo, min(lo + BLOCK, border))
         for t in range(PACK):
             centre_vector(z_bf[0][:, :, t], t, 0, BLOCK)
         quantise_z(0)
         for b in range(1, BLOCKS):
             lo, hi = b * BLOCK, (b + 1) * BLOCK
-            for t in range(2):
-                if lo < border:
-                    centre_pairs(centre_scalar, t, lo, min(hi, border))
-                if hi > border:
-                    centre_pairs(centre_vector, t, max(lo, border), hi)
-            for t in range(2, PACK):
-                centre_pairs(centre_vector, t, lo, hi)
-        for b in range(1, BLOCKS):
+            for t in range(PACK):
+                first = max(lo, border) if t < 2 else lo
+                if first < hi:
+                    centre_pairs(centre_vector, t, first, hi)
             weave(b, nc.scalar.copy if b == 2 else nc.vector.tensor_copy)
             quantise_z(b)
         for b in range(BLOCKS):

@@ -26,7 +26,7 @@ BLOCKS = S // BLOCK
 OUT_TILES = N // P
 WARM_ROWS = 32
 WARM_COLUMNS = (512, 512, 128)
-SCALAR_ENTRIES = 320
+SCALAR_ENTRIES = 256
 SCALAR_EMPTIES = 1
 STORE_FROM = {0: 0, 1: 1, 3: 2}
 
@@ -180,19 +180,23 @@ def tile_picked_deepset_none_p_kernel(tc, x_words, x_scales, w1, w2_words, w2_sc
                     stored = slice(STORE_FROM[b] * BLOCK, (b + 1) * BLOCK)
                     nc.sync.dma_start(out=out_rows[:, a, stored], in_=result[a][:, stored])
 
-        border = BLOCK + SCALAR_ENTRIES
-        for lo in range(BLOCK, border, BLOCK):
+        border = S - SCALAR_ENTRIES
+
+        def stretches(lo, hi):
+            return [(max(lo, c), min(hi, c + BLOCK)) for c in range(lo - lo % BLOCK, hi, BLOCK)]
+
+        for lo, hi in stretches(border, S):
             for t in range(2):
-                centre_pairs(centre_scalar, t, lo, min(lo + BLOCK, border))
+                centre_pairs(centre_scalar, t, lo, hi)
         for t in range(PACK):
             centre_vector(z_bf[0][:, :, t], t, 0, BLOCK)
         quantise_z(0)
+        for lo, hi in stretches(BLOCK, border):
+            for t in range(2):
+                centre_pairs(centre_vector, t, lo, hi)
         for b in range(1, BLOCKS):
-            lo, hi = b * BLOCK, (b + 1) * BLOCK
-            for t in range(PACK):
-                first = max(lo, border) if t < 2 else lo
-                if first < hi:
-                    centre_pairs(centre_vector, t, first, hi)
+            for t in range(2, PACK):
+                centre_pairs(centre_vector, t, b * BLOCK, (b + 1) * BLOCK)
             weave(b, nc.scalar.copy if b == 2 else nc.vector.tensor_copy)
             quantise_z(b)
         for b in range(BLOCKS):

@@ -26,7 +26,6 @@ BLOCKS = S // BLOCK
 OUT_TILES = N // P
 WARM_ROWS = 32
 WARM_COLUMNS = (512, 512, 128)
-SCALAR_ENTRIES = 256
 SCALAR_EMPTIES = 1
 STORE_FROM = {0: 0, 1: 1, 3: 2}
 
@@ -180,24 +179,20 @@ def tile_picked_deepset_none_p_kernel(tc, x_words, x_scales, w1, w2_words, w2_sc
                     stored = slice(STORE_FROM[b] * BLOCK, (b + 1) * BLOCK)
                     nc.sync.dma_start(out=out_rows[:, a, stored], in_=result[a][:, stored])
 
-        border = S - SCALAR_ENTRIES
-
-        def stretches(lo, hi):
-            return [(max(lo, c), min(hi, c + BLOCK)) for c in range(lo - lo % BLOCK, hi, BLOCK)]
-
-        for lo, hi in stretches(border, S):
-            for t in range(2):
-                centre_pairs(centre_scalar, t, lo, hi)
+        last_tile, last_block = PACK - 1, BLOCKS - 1
+        for t in range(PACK):
+            centre_pairs(centre_scalar, t, last_block * BLOCK, S)
+        weave(last_block, nc.scalar.copy)
         for t in range(PACK):
             centre_vector(z_bf[0][:, :, t], t, 0, BLOCK)
         quantise_z(0)
-        for lo, hi in stretches(BLOCK, border):
-            for t in range(2):
-                centre_pairs(centre_vector, t, lo, hi)
-        for b in range(1, BLOCKS):
-            for t in range(2, PACK):
+        for t in range(last_tile):
+            for b in range(1, last_block):
                 centre_pairs(centre_vector, t, b * BLOCK, (b + 1) * BLOCK)
-            weave(b, nc.scalar.copy if b == 2 else nc.vector.tensor_copy)
+        for b in range(1, last_block):
+            centre_pairs(centre_vector, last_tile, b * BLOCK, (b + 1) * BLOCK)
+            weave(b, nc.vector.tensor_copy)
             quantise_z(b)
+        quantise_z(last_block)
         for b in range(BLOCKS):
             second_product(b)

@@ -27,6 +27,7 @@ OUT_TILES = N // P
 WARM_ROWS = 32
 WARM_COLUMNS = (512, 512, 128)
 SCALAR_EMPTIES = 1
+VECTOR_CASTS = (40, 24)
 STORE_FROM = {0: 0, 1: 1, 3: 2}
 
 
@@ -36,41 +37,42 @@ def tile_picked_deepset_none_p_kernel(tc, x_words, x_scales, w1, w2_words, w2_sc
         sb = ctx.enter_context(tc.tile_pool(name="sb", bufs=1))
         ps = ctx.enter_context(tc.psum_pool(name="ps", bufs=1))
 
+        shared = ctx.enter_context(tc.tile_pool(name="shared", bufs=1))
+
         offsets = sb.tile([P, S // LIST_ROWS], U16, name="offsets")
-        w1_early = [sb.tile([P, 2, H // 2], F32, name="w1_early%d" % side, align_bytes=64) for side in range(2)]
-        w1_late = [sb.tile([P, 2, H // 2], F32, name="w1_late%d" % side, align_bytes=64) for side in range(2)]
-        xw = sb.tile([P, T], I32, name="xw", align_bytes=64)
-        xs = sb.tile([P, T], U8, name="xs", align_bytes=64)
-        w2w = sb.tile([P, N], I32, name="w2w", align_bytes=64)
-        w2s = sb.tile([P, N], U8, name="w2s", align_bytes=64)
+        w1_side = [sb.tile([P, PACK, H // 2], F32, name="w1_side%d" % side, align_bytes=64) for side in range(2)]
 
-        nc.vector.memset(xs[:].bitcast(I32), 0)
-        nc.vector.memset(w2s[:].bitcast(I32), 0)
+        w2w = shared.tile([P, N], I32, name="w2w", align_bytes=64, offset=0)
+        xs = shared.tile([P, T], U8, name="xs", align_bytes=64, offset=512)
+        w2s = shared.tile([P, N], U8, name="w2s", align_bytes=64, offset=1024)
+        picked_words = shared.tile([P, S], U32, name="picked_words", align_bytes=64, offset=1280)
+        xw = shared.tile([P, T], I32, name="xw", align_bytes=64, offset=3328)
+        w1_bf = [
+            [shared.tile([P, 2, P // 2, PACK], BF16, name="w1_bf%d%d" % (v, side), align_bytes=64, offset=3328 + 1024 * v) for side in range(2)]
+            for v in range(2)
+        ]
+        w1_codes = [shared.tile([P, P], U32, name="w1_codes%d" % t, align_bytes=64, offset=5376 + 512 * t) for t in range(PACK)]
 
-        def load_scale_rows(tile, rows):
+        def load_scale_rows(queue, tile, rows):
             for q in range(QUADRANTS):
-                nc.sync.dma_start(out=tile[32 * q : 32 * q + 4, :].bitcast(I32), in_=rows[4 * q : 4 * q + 4, :].bitcast(I32))
+                queue.dma_start(out=tile[32 * q : 32 * q + 4, :].bitcast(I32), in_=rows[4 * q : 4 * q + 4, :].bitcast(I32))
 
         w1_rows = w1.rearrange("(p r) i -> p r i", r=PACK)
         x_rows = x_words[0].rearrange("p c r -> p (c r)").bitcast(I32)
 
-        def load_early(side):
-            nc.sync.dma_start(out=w1_early[side][:], in_=w1_rows[:, 0:2, side * H // 2 : (side + 1) * H // 2])
-
+        nc.vector.memset(xs[:].bitcast(I32), 0)
+        load_scale_rows(nc.scalar, xs, x_scales[0])
         nc.sync.dma_start(offsets[:], offs)
         nc.sync.dma_start(out=xw[:], in_=x_rows)
-        load_early(0)
-        load_scale_rows(xs, x_scales[0])
-        load_early(1)
         for side in range(2):
-            nc.sync.dma_start(out=w1_late[side][:], in_=w1_rows[:, 2:4, side * H // 2 : (side + 1) * H // 2])
-        nc.sync.dma_start(out=w2w[:], in_=w2_words[0].rearrange("p c r -> p (c r)").bitcast(I32))
-        load_scale_rows(w2s, w2_scales[0])
+            nc.sync.dma_start(out=w1_side[side][:], in_=w1_rows[:, :, side * H // 2 : (side + 1) * H // 2])
 
-        picked_words = sb.tile([P, S], U32, name="picked_words", align_bytes=64)
-        nc.vector.tensor_copy(picked_words[:], xw[:].bitcast(U32).indirect(offsets[:]))
         picked_scales = sb.tile([P, S], U8, name="picked_scales", align_bytes=64)
         nc.vector.tensor_copy(picked_scales[:], xs[:].indirect(offsets[:]))
+        nc.vector.memset(w2s[:].bitcast(I32), 0)
+        nc.sync.dma_start(out=w2w[:], in_=w2_words[0].rearrange("p c r -> p (c r)").bitcast(I32))
+        load_scale_rows(nc.sync, w2s, w2_scales[0])
+        nc.vector.tensor_copy(picked_words[:], xw[:].bitcast(U32).indirect(offsets[:]))
         word_bytes = picked_words[:].bitcast(U8)
 
         warm_bank = ps.tile([WARM_ROWS, S], F32, name="warm_bank", tag="fresh0")
@@ -85,41 +87,36 @@ def tile_picked_deepset_none_p_kernel(tc, x_words, x_scales, w1, w2_words, w2_sc
                 stop=True,
             )
 
-        w1_bf = [sb.tile([P, 2, P, PACK], BF16, name="w1_bf%d" % v, align_bytes=64) for v in range(2)]
-        cast_out = [w1_bf[v][:].rearrange("p e m r -> p m r e") for v in range(2)]
-
-        def cast_early(side, v):
-            source = w1_early[side][:].rearrange("p r (m t) -> p m r t", t=PACK)
-            nc.scalar.copy(out=cast_out[v][:, side * P // 2 : (side + 1) * P // 2, 0:2], in_=source[:, :, :, 2 * v : 2 * v + 2])
-
-        def cast_late(side, v, copy):
-            source = w1_late[side][:].rearrange("p r (m t) -> p m r t", t=PACK)
-            copy(out=cast_out[v][:, side * P // 2 : (side + 1) * P // 2, 2:4], in_=source[:, :, :, 2 * v : 2 * v + 2])
-
-        for side in range(2):
-            for v in range(2):
-                cast_early(side, v)
-        cast_late(0, 0, nc.vector.tensor_copy)
-        cast_late(0, 1, nc.scalar.copy)
-        last_quarter = w1_late[1][:].rearrange("p r (m t) -> p m r t", t=PACK)
-        for t in range(2):
-            nc.vector.tensor_copy(out=cast_out[0][:, P // 2 :, 2:4, t], in_=last_quarter[:, :, :, t])
-        cast_late(1, 1, nc.scalar.copy)
-
-        w1_codes = [sb.tile([P, P], U32, name="w1_codes%d" % t, align_bytes=64) for t in range(PACK)]
         w1_scales = [sb.tile([P, P], U8, name="w1_scales%d" % t, align_bytes=64) for t in range(PACK)]
         h_bank = [ps.tile([P, S], F32, name="h_bank%d" % t) for t in range(PACK)]
+
+        def cast(copy, v, side, lo, hi):
+            source = w1_side[side][:].rearrange("p r (m t) -> p m r t", t=PACK)
+            copy(out=w1_bf[v][side][:].rearrange("p e m r -> p m r e")[:, lo:hi], in_=source[:, lo:hi, :, 2 * v : 2 * v + 2])
+
+        def quantise_w1(t, side):
+            half = slice(side * P // 2, (side + 1) * P // 2)
+            nc.vector.quantize_mx(out=w1_codes[t][:, half].bitcast(FP8X4), scales=w1_scales[t][:, half], in_=w1_bf[t // 2][side][:, t % 2].rearrange("p m r -> p (m r)"))
+
+        cast(nc.vector.tensor_copy, 0, 0, 0, P // 2)
+        cast(nc.vector.tensor_copy, 1, 0, 0, VECTOR_CASTS[1])
+        cast(nc.scalar.copy, 1, 0, VECTOR_CASTS[1], P // 2)
         for t in range(PACK):
-            nc.vector.quantize_mx(out=w1_codes[t][:].bitcast(FP8X4), scales=w1_scales[t][:], in_=w1_bf[t // 2][:, t % 2].rearrange("p m r -> p (m r)"))
-            nc.tensor.matmul_mx(
-                out=h_bank[t][:],
-                lhsT=w1_codes[t][:].bitcast(FP8X4),
-                lhsT_scale=w1_scales[t][:],
-                rhs=picked_words[:].bitcast(FP8X4),
-                rhs_scale=picked_scales[:],
-                start=True,
-                stop=True,
-            )
+            quantise_w1(t, 0)
+        for v in range(2):
+            cast(nc.vector.tensor_copy, v, 1, 0, VECTOR_CASTS[v])
+            cast(nc.scalar.copy, v, 1, VECTOR_CASTS[v], P // 2)
+            for t in range(2 * v, 2 * v + 2):
+                quantise_w1(t, 1)
+                nc.tensor.matmul_mx(
+                    out=h_bank[t][:],
+                    lhsT=w1_codes[t][:].bitcast(FP8X4),
+                    lhsT_scale=w1_scales[t][:],
+                    rhs=picked_words[:].bitcast(FP8X4),
+                    rhs_scale=picked_scales[:],
+                    start=True,
+                    stop=True,
+                )
 
         h_scaled = [sb.tile([P, S], F32, name="h_scaled%d" % t, align_bytes=64) for t in range(PACK)]
         minus_mean = [sb.tile([P, 1], F32, name="minus_mean%d" % t) for t in range(PACK)]

@@ -27,7 +27,8 @@ OUT_TILES = N // P
 WARM_ROWS = 32
 WARM_COLUMNS = (512, 512, 128)
 SCALAR_EMPTIES = 1
-VECTOR_CASTS = (40, 24)
+HALF = P // 2
+VECTOR_CASTS = (44, 40)
 STORE_FROM = {0: 0, 1: 1, 3: 2}
 
 
@@ -37,42 +38,35 @@ def tile_picked_deepset_none_p_kernel(tc, x_words, x_scales, w1, w2_words, w2_sc
         sb = ctx.enter_context(tc.tile_pool(name="sb", bufs=1))
         ps = ctx.enter_context(tc.psum_pool(name="ps", bufs=1))
 
-        shared = ctx.enter_context(tc.tile_pool(name="shared", bufs=1))
-
         offsets = sb.tile([P, S // LIST_ROWS], U16, name="offsets")
         w1_side = [sb.tile([P, PACK, H // 2], F32, name="w1_side%d" % side, align_bytes=64) for side in range(2)]
+        xw = sb.tile([P, T], I32, name="xw", align_bytes=64)
+        xs = sb.tile([P, T], U8, name="xs", align_bytes=64)
+        w2w = sb.tile([P, N], I32, name="w2w", align_bytes=64)
+        w2s = sb.tile([P, N], U8, name="w2s", align_bytes=64)
 
-        w2w = shared.tile([P, N], I32, name="w2w", align_bytes=64, offset=0)
-        xs = shared.tile([P, T], U8, name="xs", align_bytes=64, offset=512)
-        w2s = shared.tile([P, N], U8, name="w2s", align_bytes=64, offset=1024)
-        picked_words = shared.tile([P, S], U32, name="picked_words", align_bytes=64, offset=1280)
-        xw = shared.tile([P, T], I32, name="xw", align_bytes=64, offset=3328)
-        w1_bf = [
-            [shared.tile([P, 2, P // 2, PACK], BF16, name="w1_bf%d%d" % (v, side), align_bytes=64, offset=3328 + 1024 * v) for side in range(2)]
-            for v in range(2)
-        ]
-        w1_codes = [shared.tile([P, P], U32, name="w1_codes%d" % t, align_bytes=64, offset=5376 + 512 * t) for t in range(PACK)]
+        nc.vector.memset(xs[:].bitcast(I32), 0)
+        nc.vector.memset(w2s[:].bitcast(I32), 0)
 
-        def load_scale_rows(queue, tile, rows):
+        def load_scale_rows(tile, rows):
             for q in range(QUADRANTS):
-                queue.dma_start(out=tile[32 * q : 32 * q + 4, :].bitcast(I32), in_=rows[4 * q : 4 * q + 4, :].bitcast(I32))
+                nc.sync.dma_start(out=tile[32 * q : 32 * q + 4, :].bitcast(I32), in_=rows[4 * q : 4 * q + 4, :].bitcast(I32))
 
         w1_rows = w1.rearrange("(p r) i -> p r i", r=PACK)
         x_rows = x_words[0].rearrange("p c r -> p (c r)").bitcast(I32)
 
-        nc.vector.memset(xs[:].bitcast(I32), 0)
-        load_scale_rows(nc.scalar, xs, x_scales[0])
         nc.sync.dma_start(offsets[:], offs)
         nc.sync.dma_start(out=xw[:], in_=x_rows)
+        load_scale_rows(xs, x_scales[0])
         for side in range(2):
             nc.sync.dma_start(out=w1_side[side][:], in_=w1_rows[:, :, side * H // 2 : (side + 1) * H // 2])
+        nc.sync.dma_start(out=w2w[:], in_=w2_words[0].rearrange("p c r -> p (c r)").bitcast(I32))
+        load_scale_rows(w2s, w2_scales[0])
 
+        picked_words = sb.tile([P, S], U32, name="picked_words", align_bytes=64)
+        nc.vector.tensor_copy(picked_words[:], xw[:].bitcast(U32).indirect(offsets[:]))
         picked_scales = sb.tile([P, S], U8, name="picked_scales", align_bytes=64)
         nc.vector.tensor_copy(picked_scales[:], xs[:].indirect(offsets[:]))
-        nc.vector.memset(w2s[:].bitcast(I32), 0)
-        nc.sync.dma_start(out=w2w[:], in_=w2_words[0].rearrange("p c r -> p (c r)").bitcast(I32))
-        load_scale_rows(nc.sync, w2s, w2_scales[0])
-        nc.vector.tensor_copy(picked_words[:], xw[:].bitcast(U32).indirect(offsets[:]))
         word_bytes = picked_words[:].bitcast(U8)
 
         warm_bank = ps.tile([WARM_ROWS, S], F32, name="warm_bank", tag="fresh0")
@@ -87,36 +81,37 @@ def tile_picked_deepset_none_p_kernel(tc, x_words, x_scales, w1, w2_words, w2_sc
                 stop=True,
             )
 
+        w1_bf = [sb.tile([P, 2, P, PACK], BF16, name="w1_bf%d" % v, align_bytes=64) for v in range(2)]
+        w1_codes = [sb.tile([P, P], U32, name="w1_codes%d" % t, align_bytes=64) for t in range(PACK)]
         w1_scales = [sb.tile([P, P], U8, name="w1_scales%d" % t, align_bytes=64) for t in range(PACK)]
         h_bank = [ps.tile([P, S], F32, name="h_bank%d" % t) for t in range(PACK)]
 
         def cast(copy, v, side, lo, hi):
             source = w1_side[side][:].rearrange("p r (m t) -> p m r t", t=PACK)
-            copy(out=w1_bf[v][side][:].rearrange("p e m r -> p m r e")[:, lo:hi], in_=source[:, lo:hi, :, 2 * v : 2 * v + 2])
+            first = side * HALF
+            copy(out=w1_bf[v][:].rearrange("p e m r -> p m r e")[:, first + lo : first + hi], in_=source[:, lo:hi, :, 2 * v : 2 * v + 2])
 
-        def quantise_w1(t, side):
-            half = slice(side * P // 2, (side + 1) * P // 2)
-            nc.vector.quantize_mx(out=w1_codes[t][:, half].bitcast(FP8X4), scales=w1_scales[t][:, half], in_=w1_bf[t // 2][side][:, t % 2].rearrange("p m r -> p (m r)"))
+        def quantise_w1(t, lo, hi):
+            nc.vector.quantize_mx(out=w1_codes[t][:, lo:hi].bitcast(FP8X4), scales=w1_scales[t][:, lo:hi], in_=w1_bf[t // 2][:, t % 2, lo:hi].rearrange("p m r -> p (m r)"))
 
-        cast(nc.vector.tensor_copy, 0, 0, 0, P // 2)
-        cast(nc.vector.tensor_copy, 1, 0, 0, VECTOR_CASTS[1])
-        cast(nc.scalar.copy, 1, 0, VECTOR_CASTS[1], P // 2)
-        for t in range(PACK):
-            quantise_w1(t, 0)
+        for v in range(2):
+            cast(nc.scalar.copy, v, 0, 0, HALF)
+        for t in range(2):
+            quantise_w1(t, 0, HALF)
         for v in range(2):
             cast(nc.vector.tensor_copy, v, 1, 0, VECTOR_CASTS[v])
-            cast(nc.scalar.copy, v, 1, VECTOR_CASTS[v], P // 2)
-            for t in range(2 * v, 2 * v + 2):
-                quantise_w1(t, 1)
-                nc.tensor.matmul_mx(
-                    out=h_bank[t][:],
-                    lhsT=w1_codes[t][:].bitcast(FP8X4),
-                    lhsT_scale=w1_scales[t][:],
-                    rhs=picked_words[:].bitcast(FP8X4),
-                    rhs_scale=picked_scales[:],
-                    start=True,
-                    stop=True,
-                )
+            cast(nc.scalar.copy, v, 1, VECTOR_CASTS[v], HALF)
+        for t in range(PACK):
+            quantise_w1(t, HALF if t < 2 else 0, P)
+            nc.tensor.matmul_mx(
+                out=h_bank[t][:],
+                lhsT=w1_codes[t][:].bitcast(FP8X4),
+                lhsT_scale=w1_scales[t][:],
+                rhs=picked_words[:].bitcast(FP8X4),
+                rhs_scale=picked_scales[:],
+                start=True,
+                stop=True,
+            )
 
         h_scaled = [sb.tile([P, S], F32, name="h_scaled%d" % t, align_bytes=64) for t in range(PACK)]
         minus_mean = [sb.tile([P, 1], F32, name="minus_mean%d" % t) for t in range(PACK)]

@@ -55,8 +55,8 @@ def tile_picked_deepset_none_p_kernel(tc, x_words, x_scales, w1, w2_words, w2_sc
         w1_rows = w1.rearrange("(p r) i -> p r i", r=PACK)
         x_rows = x_words[0].rearrange("p c r -> p (c r)").bitcast(I32)
 
-        nc.sync.dma_start(offsets[:], offs)
         nc.sync.dma_start(out=xw[:], in_=x_rows)
+        nc.sync.dma_start(offsets[:], offs)
         load_scale_rows(xs, x_scales[0])
         for side in range(2):
             nc.sync.dma_start(out=w1_side[side][:], in_=w1_rows[:, :, side * H // 2 : (side + 1) * H // 2])
@@ -122,7 +122,9 @@ def tile_picked_deepset_none_p_kernel(tc, x_words, x_scales, w1, w2_words, w2_sc
                 nc.scalar.activation(out=h_scaled[t][:], in_=h_bank[t][:], func=COPY, scale=-1.0 / S, accum_out=minus_mean[t][:])
 
         z_bf = [sb.tile([P, BLOCK, PACK], BF16, name="z_bf%d" % b, align_bytes=64) for b in range(BLOCKS)]
-        z_pairs = {b: sb.tile([P, 2, BLOCK, 2], BF16, name="z_pairs%d" % b, align_bytes=64) for b in range(1, BLOCKS)}
+        middle_pairs = sb.tile([P, 2, 2 * BLOCK, 2], BF16, name="middle_pairs", align_bytes=64)
+        last_pairs = sb.tile([P, 2, BLOCK, 2], BF16, name="last_pairs", align_bytes=64)
+        z_pairs = {1: middle_pairs[:, :, :BLOCK], 2: middle_pairs[:, :, BLOCK:], 3: last_pairs[:]}
         z_codes = [sb.tile([P, BLOCK], U32, name="z_codes%d" % b, align_bytes=64) for b in range(BLOCKS)]
         z_scales = [sb.tile([P, BLOCK], U8, name="z_scales%d" % b, align_bytes=64) for b in range(BLOCKS)]
 
@@ -139,7 +141,7 @@ def tile_picked_deepset_none_p_kernel(tc, x_words, x_scales, w1, w2_words, w2_sc
         def weave(b, copy):
             copy(
                 out=z_bf[b][:].rearrange("p c r -> p (c r)").bitcast(F32).rearrange("p (c v) -> p c v", v=2),
-                in_=z_pairs[b][:].rearrange("p v c e -> p v (c e)").bitcast(F32).rearrange("p v c -> p c v"),
+                in_=z_pairs[b].rearrange("p v c e -> p v (c e)").bitcast(F32).rearrange("p v c -> p c v"),
             )
 
         def quantise_z(b):
@@ -179,8 +181,7 @@ def tile_picked_deepset_none_p_kernel(tc, x_words, x_scales, w1, w2_words, w2_sc
             centre_vector(z_bf[0][:, :, t], t, 0, BLOCK)
         quantise_z(0)
         for t in range(last_tile):
-            for b in range(1, last_block):
-                centre_pairs(centre_vector, t, b * BLOCK, (b + 1) * BLOCK)
+            centre_vector(middle_pairs[:, t // 2, :, t % 2], t, BLOCK, last_block * BLOCK)
         for b in range(1, last_block):
             centre_pairs(centre_vector, last_tile, b * BLOCK, (b + 1) * BLOCK)
             weave(b, nc.vector.tensor_copy)

@@ -29,7 +29,7 @@ WARM_COLUMNS = (512, 512, 128)
 SCALAR_EMPTIES = 1
 HALF = P // 2
 VECTOR_CASTS = (44, 40)
-STORE_FROM = {0: 0, 1: 1, 3: 2}
+STORE_FROM = ({0: 0, 1: 1, 2: 2, 3: 3}, {0: 0, 1: 1, 3: 2})
 
 
 def tile_picked_deepset_none_p_kernel(tc, x_words, x_scales, w1, w2_words, w2_scales, offs, out):
@@ -169,8 +169,8 @@ def tile_picked_deepset_none_p_kernel(tc, x_words, x_scales, w1, w2_words, w2_sc
                     nc.scalar.copy(out=result[a][:, entries], in_=acc[:])
                 else:
                     nc.vector.tensor_copy(out=result[a][:, entries], in_=acc[:])
-                if b in STORE_FROM:
-                    stored = slice(STORE_FROM[b] * BLOCK, (b + 1) * BLOCK)
+                if b in STORE_FROM[a]:
+                    stored = slice(STORE_FROM[a][b] * BLOCK, (b + 1) * BLOCK)
                     nc.sync.dma_start(out=out_rows[:, a, stored], in_=result[a][:, stored])
 
         last_tile, last_block = PACK - 1, BLOCKS - 1

@@ -27,8 +27,10 @@ OUT_TILES = N // P
 WARM_ROWS = 32
 WARM_COLUMNS = (512, 512, 128)
 SCALAR_EMPTIES = 1
+VECTOR_WEAVES = 2
 HALF = P // 2
-VECTOR_CASTS = (44, 40)
+VECTOR_CASTS = (16, 40)
+SCALAR_EARLY = 52
 STORE_FROM = ({0: 0, 1: 1, 2: 2, 3: 3}, {0: 0, 1: 1, 3: 2})
 
 
@@ -94,13 +96,15 @@ def tile_picked_deepset_none_p_kernel(tc, x_words, x_scales, w1, w2_words, w2_sc
         def quantise_w1(t, lo, hi):
             nc.vector.quantize_mx(out=w1_codes[t][:, lo:hi].bitcast(FP8X4), scales=w1_scales[t][:, lo:hi], in_=w1_bf[t // 2][:, t % 2, lo:hi].rearrange("p m r -> p (m r)"))
 
-        for v in range(2):
-            cast(nc.scalar.copy, v, 0, 0, HALF)
+        cast(nc.scalar.copy, 0, 0, 0, HALF)
+        cast(nc.scalar.copy, 1, 0, 0, SCALAR_EARLY)
         for t in range(2):
             quantise_w1(t, 0, HALF)
-        for v in range(2):
-            cast(nc.vector.tensor_copy, v, 1, 0, VECTOR_CASTS[v])
-            cast(nc.scalar.copy, v, 1, VECTOR_CASTS[v], HALF)
+        cast(nc.vector.tensor_copy, 0, 1, 0, VECTOR_CASTS[0])
+        cast(nc.scalar.copy, 0, 1, VECTOR_CASTS[0], HALF)
+        cast(nc.scalar.copy, 1, 0, SCALAR_EARLY, HALF)
+        cast(nc.vector.tensor_copy, 1, 1, 0, VECTOR_CASTS[1])
+        cast(nc.scalar.copy, 1, 1, VECTOR_CASTS[1], HALF)
         for t in range(PACK):
             quantise_w1(t, HALF if t < 2 else 0, P)
             nc.tensor.matmul_mx(
@@ -122,9 +126,10 @@ def tile_picked_deepset_none_p_kernel(tc, x_words, x_scales, w1, w2_words, w2_sc
                 nc.scalar.activation(out=h_scaled[t][:], in_=h_bank[t][:], func=COPY, scale=-1.0 / S, accum_out=minus_mean[t][:])
 
         z_bf = [sb.tile([P, BLOCK, PACK], BF16, name="z_bf%d" % b, align_bytes=64) for b in range(BLOCKS)]
-        middle_pairs = sb.tile([P, 2, 2 * BLOCK, 2], BF16, name="middle_pairs", align_bytes=64)
+        middle_pairs = sb.tile([P, 2, 3 * BLOCK, 2], BF16, name="middle_pairs", align_bytes=64)
         last_pairs = sb.tile([P, 2, BLOCK, 2], BF16, name="last_pairs", align_bytes=64)
-        z_pairs = {1: middle_pairs[:, :, :BLOCK], 2: middle_pairs[:, :, BLOCK:], 3: last_pairs[:]}
+        z_pairs = {b: middle_pairs[:, :, b * BLOCK : (b + 1) * BLOCK] for b in range(3)}
+        z_pairs[3] = last_pairs[:]
         z_codes = [sb.tile([P, BLOCK], U32, name="z_codes%d" % b, align_bytes=64) for b in range(BLOCKS)]
         z_scales = [sb.tile([P, BLOCK], U8, name="z_scales%d" % b, align_bytes=64) for b in range(BLOCKS)]
 
@@ -176,16 +181,13 @@ def tile_picked_deepset_none_p_kernel(tc, x_words, x_scales, w1, w2_words, w2_sc
         last_tile, last_block = PACK - 1, BLOCKS - 1
         for t in range(PACK):
             centre_pairs(centre_scalar, t, last_block * BLOCK, S)
-        weave(last_block, nc.scalar.copy)
-        for t in range(PACK):
-            centre_vector(z_bf[0][:, :, t], t, 0, BLOCK)
-        quantise_z(0)
         for t in range(last_tile):
-            centre_vector(middle_pairs[:, t // 2, :, t % 2], t, BLOCK, last_block * BLOCK)
-        for b in range(1, last_block):
+            centre_vector(middle_pairs[:, t // 2, :, t % 2], t, 0, last_block * BLOCK)
+        for b in range(last_block):
             centre_pairs(centre_vector, last_tile, b * BLOCK, (b + 1) * BLOCK)
-            weave(b, nc.vector.tensor_copy)
+            weave(b, nc.vector.tensor_copy if b < VECTOR_WEAVES else nc.scalar.copy)
             quantise_z(b)
+        weave(last_block, nc.scalar.copy)
         quantise_z(last_block)
         for b in range(BLOCKS):
             second_product(b)

@@ -26,12 +26,11 @@ BLOCKS = S // BLOCK
 OUT_TILES = N // P
 WARM_ROWS = 32
 WARM_COLUMNS = (512, 512, 128)
-SCALAR_EMPTIES = 1
 VECTOR_WEAVES = 2
 HALF = P // 2
 VECTOR_CASTS = (16, 40)
 SCALAR_EARLY = 52
-STORE_FROM = ({0: 0, 1: 1, 2: 2, 3: 3}, {0: 0, 1: 1, 3: 2})
+STORE_FROM = ({0: 0, 1: 1, 3: 2}, {1: 0, 3: 2})
 
 
 def tile_picked_deepset_none_p_kernel(tc, x_words, x_scales, w1, w2_words, w2_scales, offs, out):
@@ -170,7 +169,7 @@ def tile_picked_deepset_none_p_kernel(tc, x_words, x_scales, w1, w2_words, w2_sc
                     start=True,
                     stop=True,
                 )
-                if a == 0 or b < SCALAR_EMPTIES:
+                if a == 0:
                     nc.scalar.copy(out=result[a][:, entries], in_=acc[:])
                 else:
                     nc.vector.tensor_copy(out=result[a][:, entries], in_=acc[:])

@@ -28,7 +28,7 @@ WARM_ROWS = 32
 WARM_COLUMNS = (512, 512, 128)
 VECTOR_WEAVES = 2
 HALF = P // 2
-VECTOR_CASTS = (16, 40)
+VECTOR_CASTS = (44, 40)
 SCALAR_EARLY = 52
 STORE_FROM = ({0: 0, 1: 1, 3: 2}, {1: 0, 3: 2})
 

@@ -28,8 +28,8 @@ WARM_ROWS = 32
 WARM_COLUMNS = (512, 512, 128)
 VECTOR_WEAVES = 2
 HALF = P // 2
-VECTOR_CASTS = (44, 40)
-SCALAR_EARLY = 52
+VECTOR_CASTS = (44, 56)
+SCALAR_EARLY = 16
 STORE_FROM = ({0: 0, 1: 1, 3: 2}, {1: 0, 3: 2})
 
 
@@ -59,8 +59,9 @@ def tile_picked_deepset_none_p_kernel(tc, x_words, x_scales, w1, w2_words, w2_sc
         nc.sync.dma_start(out=xw[:], in_=x_rows)
         nc.sync.dma_start(offsets[:], offs)
         load_scale_rows(xs, x_scales[0])
-        for side in range(2):
-            nc.sync.dma_start(out=w1_side[side][:], in_=w1_rows[:, :, side * H // 2 : (side + 1) * H // 2])
+        nc.sync.dma_start(out=w1_side[0][:], in_=w1_rows[:, :, : H // 2])
+        for rows in (slice(0, 2), slice(2, 4)):
+            nc.sync.dma_start(out=w1_side[1][:, rows], in_=w1_rows[:, rows, H // 2 :])
         nc.sync.dma_start(out=w2w[:], in_=w2_words[0].rearrange("p c r -> p (c r)").bitcast(I32))
         load_scale_rows(w2s, w2_scales[0])
 
@@ -92,17 +93,22 @@ def tile_picked_deepset_none_p_kernel(tc, x_words, x_scales, w1, w2_words, w2_sc
             first = side * HALF
             copy(out=w1_bf[v][:].rearrange("p e m r -> p m r e")[:, first + lo : first + hi], in_=source[:, lo:hi, :, 2 * v : 2 * v + 2])
 
+        def cast_rows(copy, rows, lo, hi):
+            source = w1_side[1][:].rearrange("p r (m t) -> p m r t", t=PACK)
+            copy(out=w1_bf[0][:].rearrange("p e m r -> p m r e")[:, HALF + lo : HALF + hi, rows], in_=source[:, lo:hi, rows, 0:2])
+
         def quantise_w1(t, lo, hi):
             nc.vector.quantize_mx(out=w1_codes[t][:, lo:hi].bitcast(FP8X4), scales=w1_scales[t][:, lo:hi], in_=w1_bf[t // 2][:, t % 2, lo:hi].rearrange("p m r -> p (m r)"))
 
         cast(nc.scalar.copy, 0, 0, 0, HALF)
-        cast(nc.scalar.copy, 1, 0, 0, SCALAR_EARLY)
+        cast_rows(nc.scalar.copy, slice(0, 2), 0, HALF)
         for t in range(2):
             quantise_w1(t, 0, HALF)
-        cast(nc.vector.tensor_copy, 0, 1, 0, VECTOR_CASTS[0])
-        cast(nc.scalar.copy, 0, 1, VECTOR_CASTS[0], HALF)
-        cast(nc.scalar.copy, 1, 0, SCALAR_EARLY, HALF)
+        cast(nc.scalar.copy, 1, 0, 0, SCALAR_EARLY)
+        cast_rows(nc.vector.tensor_copy, slice(2, 4), 0, VECTOR_CASTS[0])
+        cast_rows(nc.scalar.copy, slice(2, 4), VECTOR_CASTS[0], HALF)
         cast(nc.vector.tensor_copy, 1, 1, 0, VECTOR_CASTS[1])
+        cast(nc.scalar.copy, 1, 0, SCALAR_EARLY, HALF)
         cast(nc.scalar.copy, 1, 1, VECTOR_CASTS[1], HALF)
         for t in range(PACK):
             quantise_w1(t, HALF if t < 2 else 0, P)

from contextlib import ExitStack

import concourse.mybir as mybir

K, T, S, H, N = 512, 1024, 512, 512, 256
FLOPS = 2 * K * H * S + 2 * H * N * S

F32 = mybir.dt.float32
BF16 = mybir.dt.bfloat16
I32 = mybir.dt.int32
U32 = mybir.dt.uint32
U16 = mybir.dt.uint16
U8 = mybir.dt.uint8
FP8X4 = mybir.dt.float8_e4m3fn_x4
MULT = mybir.AluOpType.mult
ADD = mybir.AluOpType.add
COPY = mybir.ActivationFunctionType.Copy
IDENTITY = mybir.ActivationFunctionType.Identity

P = 128
PACK = 4
QUADRANTS = 4
LIST_ROWS = 16
BLOCK = 128
BLOCKS = S // BLOCK
OUT_TILES = N // P
WARM_ROWS = 32
WARM_COLUMNS = (512, 512, 128)
VECTOR_WEAVES = 2
HALF = P // 2
VECTOR_CASTS = (44, 56)
SCALAR_EARLY = 16
STORE_FROM = ({0: 0, 1: 1, 3: 2}, {1: 0, 3: 2})


def tile_picked_deepset_none_p_kernel(tc, x_words, x_scales, w1, w2_words, w2_scales, offs, out):
    nc = tc.nc
    with ExitStack() as ctx:
        sb = ctx.enter_context(tc.tile_pool(name="sb", bufs=1))
        ps = ctx.enter_context(tc.psum_pool(name="ps", bufs=1))

        offsets = sb.tile([P, S // LIST_ROWS], U16, name="offsets")
        w1_side = [sb.tile([P, PACK, H // 2], F32, name="w1_side%d" % side, align_bytes=64) for side in range(2)]
        xw = sb.tile([P, T], I32, name="xw", align_bytes=64)
        xs = sb.tile([P, T], U8, name="xs", align_bytes=64)
        w2w = sb.tile([P, N], I32, name="w2w", align_bytes=64)
        w2s = sb.tile([P, N], U8, name="w2s", align_bytes=64)

        nc.vector.memset(xs[:].bitcast(I32), 0)
        nc.vector.memset(w2s[:].bitcast(I32), 0)

        def load_scale_rows(tile, rows):
            for q in range(QUADRANTS):
                nc.sync.dma_start(out=tile[32 * q : 32 * q + 4, :].bitcast(I32), in_=rows[4 * q : 4 * q + 4, :].bitcast(I32))

        w1_rows = w1.rearrange("(p r) i -> p r i", r=PACK)
        x_rows = x_words[0].rearrange("p c r -> p (c r)").bitcast(I32)

        nc.sync.dma_start(out=xw[:], in_=x_rows)
        nc.sync.dma_start(offsets[:], offs)
        load_scale_rows(xs, x_scales[0])
        nc.sync.dma_start(out=w1_side[0][:], in_=w1_rows[:, :, : H // 2])
        for rows in (slice(0, 2), slice(2, 4)):
            nc.sync.dma_start(out=w1_side[1][:, rows], in_=w1_rows[:, rows, H // 2 :])
        nc.sync.dma_start(out=w2w[:], in_=w2_words[0].rearrange("p c r -> p (c r)").bitcast(I32))
        load_scale_rows(w2s, w2_scales[0])

        picked_words = sb.tile([P, S], U32, name="picked_words", align_bytes=64)
        nc.vector.tensor_copy(picked_words[:], xw[:].bitcast(U32).indirect(offsets[:]))
        picked_scales = sb.tile([P, S], U8, name="picked_scales", align_bytes=64)
        nc.vector.tensor_copy(picked_scales[:], xs[:].indirect(offsets[:]))
        word_bytes = picked_words[:].bitcast(U8)

        warm_bank = ps.tile([WARM_ROWS, S], F32, name="warm_bank", tag="fresh0")
        for columns in WARM_COLUMNS:
            nc.tensor.matmul_mx(
                out=warm_bank[:, :columns],
                lhsT=picked_words[:, :WARM_ROWS].bitcast(FP8X4),
                lhsT_scale=word_bytes[:, :WARM_ROWS],
                rhs=picked_words[:, :columns].bitcast(FP8X4),
                rhs_scale=word_bytes[:, :columns],
                start=True,
                stop=True,
            )

        w1_bf = [sb.tile([P, 2, P, PACK], BF16, name="w1_bf%d" % v, align_bytes=64) for v in range(2)]
        w1_codes = [sb.tile([P, P], U32, name="w1_codes%d" % t, align_bytes=64) for t in range(PACK)]
        w1_scales = [sb.tile([P, P], U8, name="w1_scales%d" % t, align_bytes=64) for t in range(PACK)]
        h_bank = [ps.tile([P, S], F32, name="h_bank%d" % t) for t in range(PACK)]

        def cast(copy, v, side, lo, hi):
            source = w1_side[side][:].rearrange("p r (m t) -> p m r t", t=PACK)
            first = side * HALF
            copy(out=w1_bf[v][:].rearrange("p e m r -> p m r e")[:, first + lo : first + hi], in_=source[:, lo:hi, :, 2 * v : 2 * v + 2])

        def cast_rows(copy, rows, lo, hi):
            source = w1_side[1][:].rearrange("p r (m t) -> p m r t", t=PACK)
            copy(out=w1_bf[0][:].rearrange("p e m r -> p m r e")[:, HALF + lo : HALF + hi, rows], in_=source[:, lo:hi, rows, 0:2])

        def quantise_w1(t, lo, hi):
            nc.vector.quantize_mx(out=w1_codes[t][:, lo:hi].bitcast(FP8X4), scales=w1_scales[t][:, lo:hi], in_=w1_bf[t // 2][:, t % 2, lo:hi].rearrange("p m r -> p (m r)"))

        cast(nc.scalar.copy, 0, 0, 0, HALF)
        cast_rows(nc.scalar.copy, slice(0, 2), 0, HALF)
        for t in range(2):
            quantise_w1(t, 0, HALF)
        cast(nc.scalar.copy, 1, 0, 0, SCALAR_EARLY)
        cast_rows(nc.vector.tensor_copy, slice(2, 4), 0, VECTOR_CASTS[0])
        cast_rows(nc.scalar.copy, slice(2, 4), VECTOR_CASTS[0], HALF)
        cast(nc.vector.tensor_copy, 1, 1, 0, VECTOR_CASTS[1])
        cast(nc.scalar.copy, 1, 0, SCALAR_EARLY, HALF)
        cast(nc.scalar.copy, 1, 1, VECTOR_CASTS[1], HALF)
        for t in range(PACK):
            quantise_w1(t, HALF if t < 2 else 0, P)
            nc.tensor.matmul_mx(
                out=h_bank[t][:],
                lhsT=w1_codes[t][:].bitcast(FP8X4),
                lhsT_scale=w1_scales[t][:],
                rhs=picked_words[:].bitcast(FP8X4),
                rhs_scale=picked_scales[:],
                start=True,
                stop=True,
            )

        h_scaled = [sb.tile([P, S], F32, name="h_scaled%d" % t, align_bytes=64) for t in range(PACK)]
        minus_mean = [sb.tile([P, 1], F32, name="minus_mean%d" % t) for t in range(PACK)]
        for t in range(PACK):
            if t == 1:
                nc.vector.tensor_scalar(out=h_scaled[t][:], in0=h_bank[t][:], scalar1=-1.0 / S, scalar2=None, op0=MULT, op1=ADD, accum_out=minus_mean[t][:])
            else:
                nc.scalar.activation(out=h_scaled[t][:], in_=h_bank[t][:], func=COPY, scale=-1.0 / S, accum_out=minus_mean[t][:])

        z_bf = [sb.tile([P, BLOCK, PACK], BF16, name="z_bf%d" % b, align_bytes=64) for b in range(BLOCKS)]
        middle_pairs = sb.tile([P, 2, 3 * BLOCK, 2], BF16, name="middle_pairs", align_bytes=64)
        last_pairs = sb.tile([P, 2, BLOCK, 2], BF16, name="last_pairs", align_bytes=64)
        z_pairs = {b: middle_pairs[:, :, b * BLOCK : (b + 1) * BLOCK] for b in range(3)}
        z_pairs[3] = last_pairs[:]
        z_codes = [sb.tile([P, BLOCK], U32, name="z_codes%d" % b, align_bytes=64) for b in range(BLOCKS)]
        z_scales = [sb.tile([P, BLOCK], U8, name="z_scales%d" % b, align_bytes=64) for b in range(BLOCKS)]

        def centre_vector(dst, t, lo, hi):
            nc.vector.tensor_scalar(out=dst, in0=h_scaled[t][:, lo:hi], scalar1=-float(S), scalar2=minus_mean[t][:], op0=MULT, op1=ADD)

        def centre_scalar(dst, t, lo, hi):
            nc.scalar.activation(out=dst, in_=h_scaled[t][:, lo:hi], func=IDENTITY, scale=-float(S), bias=minus_mean[t][:])

        def centre_pairs(centre, t, lo, hi):
            b = lo // BLOCK
            centre(z_pairs[b][:, t // 2, lo - b * BLOCK : hi - b * BLOCK, t % 2], t, lo, hi)

        def weave(b, copy):
            copy(
                out=z_bf[b][:].rearrange("p c r -> p (c r)").bitcast(F32).rearrange("p (c v) -> p c v", v=2),
                in_=z_pairs[b].rearrange("p v c e -> p v (c e)").bitcast(F32).rearrange("p v c -> p c v"),
            )

        def quantise_z(b):
            nc.vector.quantize_mx(out=z_codes[b][:].bitcast(FP8X4), scales=z_scales[b][:], in_=z_bf[b][:].rearrange("p c r -> p (c r)"))

        out_banks = ["fresh0", "fresh1", "fresh2", "fresh3", "h_bank0", "h_bank1", "h_bank2", "h_bank3"]
        out_rows = out.rearrange("(a p) j -> p a j", p=P)
        result = [sb.tile([P, S], F32, name="result%d" % a, align_bytes=64) for a in range(OUT_TILES)]

        def second_product(b):
            entries = slice(b * BLOCK, (b + 1) * BLOCK)
            for a in range(OUT_TILES):
                rows = slice(a * P, (a + 1) * P)
                acc = ps.tile([P, BLOCK], F32, name="acc%d%d" % (b, a), tag=out_banks[OUT_TILES * b + a])
                nc.tensor.matmul_mx(
                    out=acc[:],
                    lhsT=w2w[:, rows].bitcast(FP8X4),
                    lhsT_scale=w2s[:, rows],
                    rhs=z_codes[b][:].bitcast(FP8X4),
                    rhs_scale=z_scales[b][:],
                    start=True,
                    stop=True,
                )
                if a == 0:
                    nc.scalar.copy(out=result[a][:, entries], in_=acc[:])
                else:
                    nc.vector.tensor_copy(out=result[a][:, entries], in_=acc[:])
                if b in STORE_FROM[a]:
                    stored = slice(STORE_FROM[a][b] * BLOCK, (b + 1) * BLOCK)
                    nc.sync.dma_start(out=out_rows[:, a, stored], in_=result[a][:, stored])

        last_tile, last_block = PACK - 1, BLOCKS - 1
        for t in range(PACK):
            centre_pairs(centre_scalar, t, last_block * BLOCK, S)
        for t in range(last_tile):
            centre_vector(middle_pairs[:, t // 2, :, t % 2], t, 0, last_block * BLOCK)
        for b in range(last_block):
            centre_pairs(centre_vector, last_tile, b * BLOCK, (b + 1) * BLOCK)
            weave(b, nc.vector.tensor_copy if b < VECTOR_WEAVES else nc.scalar.copy)
            quantise_z(b)
        weave(last_block, nc.scalar.copy)
        quantise_z(last_block)
        for b in range(BLOCKS):
            second_product(b)
